import numpy as np
import ml_dtypes


def mxq(x, axis, fmt="e4m3"):
    dtype, down = {"e4m3": (ml_dtypes.float8_e4m3fn, 7), "e5m2": (ml_dtypes.float8_e5m2, 14)}[fmt]
    v = np.moveaxis(np.asarray(x, np.float32).astype(ml_dtypes.bfloat16).astype(np.float64), axis, -1)
    blocks = v.reshape(v.shape[:-1] + (-1, 32))
    amax = np.abs(blocks).max(-1, keepdims=True)
    byte = np.maximum(np.where(amax > 0, np.frexp(amax)[1] - 1 + 127, 0) - down, 1)
    scale = np.exp2(byte - 127.0)
    codes = (blocks / scale).astype(np.float32).astype(dtype).astype(np.float64)
    return np.moveaxis((codes * scale).reshape(v.shape), -1, axis)


WIDE = False


def mx_kscale(k):
    if not WIDE:
        return np.ones(k)
    levels = np.array([10, -10, 5, -5, 0])
    if k % 512:
        return np.exp2(np.random.permutation(np.resize(levels, k // 32))).repeat(32)
    a = np.empty((k // 512, 16))
    for p in range(k // 512):
        a[p, :8] = np.random.permutation(np.resize(levels, 8))
        for g in range(8):
            far = levels[np.abs(levels - a[p, g]) >= 10]
            a[p, g + 8] = far[np.random.randint(len(far))]
    return np.exp2(a.ravel()).repeat(32)


BF16 = ml_dtypes.bfloat16


def bf(x):
    return np.asarray(x, np.float32).astype(BF16)


def f64(x):
    return np.asarray(x).astype(np.float64)


E2M1 = np.array([0.0, 0.5, 1.0, 1.5, 2.0, 3.0, 4.0, 6.0, -0.0, -0.5, -1.0, -1.5, -2.0, -3.0, -4.0, -6.0])


def pack_weight(w, fmt):
    k, n = w.shape
    w = f64(bf(w)).reshape(k // 32, 32, n)
    amax = np.abs(w).max(1)
    if fmt == "e4m3":
        byte = np.frexp(amax)[1] - 1 + 127 - 7
    else:
        mant, ex = np.frexp(amax / 6.0)
        byte = np.where(mant > 0.5, ex, ex - 1) + 127
    byte = np.clip(np.where(amax > 0, byte, 1), 1, 254)
    scaled = (w * np.exp2(127.0 - byte)[:, None, :]).reshape(k, n).astype(np.float32)
    by_word = np.ascontiguousarray(scaled.reshape(k // 512, 128, 4, n).transpose(0, 1, 3, 2))
    if fmt == "e4m3":
        words = by_word.astype(ml_dtypes.float8_e4m3fn).view(np.uint8)
    else:
        c = by_word.astype(ml_dtypes.float4_e2m1fn).view(np.uint8) & 0xF
        words = c[..., 0::2] | (c[..., 1::2] << 4)
    return np.ascontiguousarray(words), np.ascontiguousarray(byte.astype(np.uint8).reshape(k // 512, 16, n))


def unpack_weight(words, scales, fmt):
    g, p, n, _ = words.shape
    if fmt == "e4m3":
        vals = np.ascontiguousarray(words).view(ml_dtypes.float8_e4m3fn).astype(np.float64)
    else:
        nib = np.empty((g, p, n, 4), np.uint8)
        nib[..., 0::2] = words & 0xF
        nib[..., 1::2] = words >> 4
        vals = E2M1[nib]
    vals = vals * np.repeat(np.exp2(scales.astype(np.float64) - 127.0), 8, axis=1)[..., None]
    return vals.transpose(0, 1, 3, 2).reshape(g * 512, n)

def planes(Y):
    n, m = Y.shape
    b = f64(bf(Y)).reshape(n // 32, 32, m)
    amax = np.abs(b).max(1)
    byte = np.clip(np.where(amax > 0, np.frexp(amax)[1] - 1 + 127 - 7, 1), 1, 254)
    codes = (b * np.exp2(127.0 - byte)[:, None, :]).reshape(n, m).astype(np.float32).astype(ml_dtypes.float8_e4m3fn).view(np.uint8)
    words = codes.reshape(n // 512, 128, 4, m).transpose(0, 1, 3, 2)
    return np.ascontiguousarray(words), np.ascontiguousarray(byte.astype(np.uint8).reshape(n // 512, 16, m))


B, S, D, E = 2, 512, 512, 1024


def setup_inputs():
    s = mx_kscale(D)
    u = mx_kscale(D)
    t = mx_kscale(S)
    q = bf(np.random.standard_normal((B, S, D)) * 1.2 * s)
    k = bf(np.random.standard_normal((B, S, D)) * 1.2 / s)
    x = bf(np.random.standard_normal((B, S, D)) * u[None, None, :] / t[None, :, None])
    w_words, w_scales = pack_weight(np.random.standard_normal((D, E)) / np.sqrt(D) / u[:, None], "e4m3")
    return {
        "q": q,
        "k": k,
        "x": x,
        "w_words": w_words,
        "w_scales": w_scales,
        "g": bf((1.0 + 0.1 * np.random.standard_normal(S)) * t),
        "beta": bf((1.0 + 0.1 * np.random.standard_normal(E)) * np.sqrt(S) / 4.0),
        "v0": bf(np.random.standard_normal((B, S, E)) * 0.5),
    }


def centered_weights(q, k, g):
    seq = k.shape[1]
    depth = q.shape[-1]
    qq = mxq(q, 2, "e4m3")
    kq = mxq(k, 2, "e4m3")
    l = (qq @ kq.transpose(0, 2, 1)) / np.sqrt(depth)
    e = np.exp(l - l.max(-1, keepdims=True))
    p = e / e.sum(-1, keepdims=True)
    return (seq * p - 1.0) * g[None, None, :]


def core(q, k, x, w_words, w_scales, g, beta, v0):
    seq = k.shape[1]
    a = centered_weights(f64(q), f64(k), f64(g))
    v = mxq(f64(x), 2, "e4m3") @ unpack_weight(w_words, w_scales, "e4m3")
    o = (mxq(a, 2, "e4m3") @ mxq(v, 1, "e4m3")) / seq
    return f64(v0) + f64(beta)[None, None, :] * o


def reference(q, k, x, w_words, w_scales, g, beta, v0):
    R_out = core(q, k, x, w_words, w_scales, g, beta, v0)
    words, scales = planes(np.moveaxis(R_out, 2, 0).reshape(1024, -1))
    return R_out, words, scales

@@ -1,0 +1,328 @@
+from contextlib import ExitStack
+
+import concourse.mybir as mybir
+from concourse.masks import make_identity
+
+F32 = mybir.dt.float32
+BF16 = mybir.dt.bfloat16
+U32 = mybir.dt.uint32
+I32 = mybir.dt.int32
+U8 = mybir.dt.uint8
+FP8X4 = mybir.dt.float8_e4m3fn_x4
+ALU = mybir.AluOpType
+ACT = mybir.ActivationFunctionType
+AX = mybir.AxisListType
+
+B, S, D, E = 2, 512, 512, 1024
+P = 128
+FLOPS = 2 * B * S * S * D + 2 * B * S * D * E + 2 * B * S * S * E
+SCALE = D ** -0.5
+
+
+def steps():
+    return [
+        ("pk", 0, 0, 0, "S"), ("pk", 0, 1, 0, "S"), ("pq", 0, 0, 0, "S"), ("qk", 0, 0, 0, "S"),
+        ("pq", 0, 1, 0, "S"), ("qk", 0, 1, 0, "S"), ("qq", 0, 0, 0, "S"), ("qq", 0, 1, 0, "S"),
+        ("px", 0, 0, 0, "S"), ("l", 0, 0, 0, "S"), ("x", 0, 0, 0, "S"), ("l", 0, 3, 0, "S"),
+        ("l", 0, 2, 0, "S"), ("n", 0, 0, 0, "S"), ("px", 0, 1, 0, "S"), ("x", 0, 2, 0, "S"),
+        ("l", 0, 1, 0, "S"), ("qx", 0, 0, 0, "S"), ("qx", 0, 1, 0, "S"), ("x", 0, 3, 0, "S"),
+        ("n", 0, 2, 0, "S"), ("x", 0, 1, 0, "S"), ("n", 0, 3, 0, "S"), ("n", 0, 1, 0, "S"),
+        ("vm", 0, 4, 0, "S"), ("a", 0, 0, 0, "S"), ("a", 0, 2, 0, "S"), ("vm", 0, 1, 0, "S"),
+        ("vm", 0, 2, 0, "S"), ("vm", 0, 6, 0, "S"), ("vm", 0, 3, 0, "S"), ("a", 0, 1, 0, "S"),
+        ("a", 0, 3, 0, "S"), ("vm", 0, 7, 0, "S"), ("vm", 0, 5, 0, "S"), ("v0", 0, 0, 0, "V"),
+        ("vm", 0, 0, 0, "V"), ("v0", 0, 0, 1, "S"), ("at", 0, 0, 0, "V"), ("vq", 0, 0, 0, "S"),
+        ("aq", 0, 0, 0, "S"), ("at", 0, 1, 0, "S"), ("px", 1, 1, 0, "S"), ("aq", 0, 1, 0, "S"),
+        ("pq", 1, 1, 0, "S"), ("v0", 0, 1, 0, "S"), ("v0", 0, 1, 1, "S"), ("vq", 0, 1, 0, "S"),
+        ("o", 0, 0, 2, "S"), ("o", 0, 0, 1, "S"), ("o", 0, 1, 3, "S"), ("o", 0, 0, 0, "S"),
+        ("o", 0, 1, 1, "S"), ("o", 0, 0, 3, "S"), ("pq", 1, 0, 0, "S"), ("pk", 1, 1, 0, "S"),
+        ("o", 0, 1, 0, "S"), ("pk", 1, 0, 0, "S"), ("ro", 0, 0, 3, "S"), ("qq", 1, 0, 0, "S"),
+        ("qk", 1, 0, 0, "S"), ("o", 0, 1, 2, "S"), ("ro", 0, 0, 1, "S"), ("qq", 1, 1, 0, "S"),
+        ("ro", 0, 0, 0, "S"), ("px", 1, 0, 0, "S"), ("ro", 0, 1, 0, "S"), ("qk", 1, 1, 0, "S"),
+        ("qx", 1, 1, 0, "S"), ("c", 0, 0, 0, "V"), ("ro", 0, 1, 3, "S"), ("l", 1, 0, 0, "S"),
+        ("l", 1, 2, 0, "S"), ("ro", 0, 0, 2, "S"), ("x", 1, 2, 0, "S"), ("l", 1, 1, 0, "S"),
+        ("l", 1, 3, 0, "S"), ("c", 0, 1, 1, "V"), ("x", 1, 0, 0, "S"), ("n", 1, 2, 0, "S"),
+        ("x", 1, 1, 0, "S"), ("qx", 1, 0, 0, "S"), ("c", 0, 1, 0, "V"), ("x", 1, 3, 0, "S"),
+        ("vm", 1, 5, 0, "S"), ("rq", 0, 1, 1, "S"), ("n", 1, 1, 0, "S"), ("a", 1, 2, 0, "S"),
+        ("n", 1, 0, 0, "S"), ("vm", 1, 2, 0, "S"), ("ro", 0, 1, 2, "S"), ("a", 1, 1, 0, "S"),
+        ("n", 1, 3, 0, "S"), ("a", 1, 0, 0, "S"), ("vm", 1, 3, 0, "S"), ("rq", 0, 1, 0, "S"),
+        ("a", 1, 3, 0, "S"), ("vm", 1, 1, 0, "S"), ("v0", 1, 0, 1, "S"), ("vm", 1, 6, 0, "S"),
+        ("c", 0, 0, 1, "V"), ("rq", 0, 0, 0, "S"), ("vm", 1, 0, 0, "S"), ("at", 1, 0, 0, "S"),
+        ("rq", 0, 0, 1, "S"), ("vm", 1, 7, 0, "S"), ("at", 1, 1, 0, "S"), ("aq", 1, 0, 0, "S"),
+        ("vq", 1, 0, 0, "S"), ("aq", 1, 1, 0, "S"), ("vm", 1, 4, 0, "S"), ("v0", 1, 0, 0, "S"),
+        ("v0", 1, 1, 0, "S"), ("vq", 1, 1, 0, "S"), ("ro", 0, 1, 1, "S"), ("o", 1, 0, 2, "S"),
+        ("o", 1, 0, 1, "S"), ("o", 1, 0, 0, "S"), ("o", 1, 0, 3, "S"), ("v0", 1, 1, 1, "S"),
+        ("o", 1, 1, 3, "S"), ("o", 1, 1, 2, "S"), ("o", 1, 1, 0, "S"), ("ro", 1, 0, 0, "S"),
+        ("ro", 1, 0, 2, "S"), ("o", 1, 1, 1, "S"), ("c", 1, 1, 0, "V"), ("ro", 1, 0, 3, "S"),
+        ("ro", 1, 0, 1, "S"), ("c", 1, 0, 0, "V"), ("ro", 1, 1, 2, "S"), ("ro", 1, 1, 3, "S"),
+        ("ro", 1, 1, 1, "S"), ("c", 1, 0, 1, "V"), ("rq", 1, 1, 0, "S"), ("rq", 1, 0, 1, "S"),
+        ("c", 1, 1, 1, "V"), ("rq", 1, 1, 1, "S"), ("ro", 1, 1, 0, "S"), ("rq", 1, 0, 0, "S"),
+    ]
+
+
+def tile_shapedcenteredattentionvalueskip_x2_kernel(
+    tc, q, k, x, w_words, w_scales, g, beta, v0, out_0, out_1, out_2
+):
+    nc = tc.nc
+    with ExitStack() as ctx:
+        keep = ctx.enter_context(tc.tile_pool(name="keep", bufs=1))
+        two = ctx.enter_context(tc.tile_pool(name="two", bufs=2))
+        stage = ctx.enter_context(tc.tile_pool(name="stage", bufs=4))
+        psum = ctx.enter_context(tc.psum_pool(name="psum", bufs=8))
+        ctx.enter_context(tc.manual_schedule())
+
+        def bank(name):
+            return psum.tile([P, 512], F32, name=name, tag="bank")
+
+        rows = keep.tile([P, S], BF16, align_bytes=64)
+        nc.vector.memset(rows[:], 0.0)
+        ones = keep.tile([P, P], BF16, align_bytes=64)
+        nc.vector.memset(ones[:], 1.0)
+        warm = keep.tile([P, 1], F32)
+        nc.vector.memset(warm[:], 0.0)
+        nc.scalar.activation(warm[:], warm[:], ACT.Exp)
+        w_sc = keep.tile([P, E], U8, align_bytes=64)
+        nc.vector.memset(w_sc[:].bitcast(I32), 0)
+        ident = keep.tile([P, P], F32, align_bytes=64)
+        make_identity(nc, ident[:])
+
+        w_c = keep.tile([P, E], U32, align_bytes=64)
+        beta_b = keep.tile([P, 2, 4], BF16)
+        beta_c = keep.tile([P, 2, 4], F32)
+        gb = keep.tile([P, S], F32, align_bytes=64)
+        ld = {}
+        for b in range(B):
+            for op in "kqx":
+                ld[op, b] = two.tile([P, 4, D], BF16, name=op + "_sb", align_bytes=64)
+            ld["v", b] = two.tile([P, 4, E], BF16, name="v_sb", align_bytes=64)
+
+        def load(op, src, b, h):
+            order = "(t p) d -> p t d" if op in "qv" else "(p t) d -> p t d"
+            nc.sync.dma_start(
+                out=ld[op, b][:, 2 * h : 2 * h + 2, :], in_=src[b].rearrange(order, t=4)[:, 2 * h : 2 * h + 2, :]
+            )
+
+        nc.scalar.dma_start(out=rows[0:1, :], in_=g.rearrange("(o s) -> o s", o=1))
+        for op, src in (("k", k), ("q", q), ("x", x)):
+            for h in (0, 1):
+                load(op, src, 0, h)
+        for Q in range(4):
+            nc.sync.dma_start(
+                out=w_sc[32 * Q : 32 * Q + 4, :].bitcast(I32), in_=w_scales[0, 4 * Q : 4 * Q + 4, :].bitcast(I32)
+            )
+        nc.sync.dma_start(out=w_c[:].bitcast(I32), in_=w_words[0].rearrange("p n t -> p (n t)").bitcast(I32))
+        nc.sync.dma_start(out=beta_b[:], in_=beta.rearrange("(g p t) -> p g t", g=2, t=4))
+        for op, src, b in (("k", k, 1), ("q", q, 1), ("v", v0, 0), ("x", x, 1), ("v", v0, 1)):
+            for h in (0, 1):
+                load(op, src, b, h)
+
+        pg = bank("pg")
+        nc.tensor.matmul(pg[:], lhsT=ones[:], rhs=rows[:], start=True, stop=True)
+        nc.scalar.activation(gb[:], pg[:], ACT.Copy, scale=float(S))
+
+        codes = {}
+        for b in range(B):
+            for key, n in (("k", 512), ("q", 512), ("x", 512), ("a", 512), ("v", E)):
+                codes[key, b] = (
+                    two.tile([P, n], U32, name=key + "_c", align_bytes=64),
+                    two.tile([P, n], U8, name=key + "_s", align_bytes=64),
+                )
+            codes["y", b] = (
+                two.tile([P, 2, 512], U32, name="y_c", align_bytes=64),
+                two.tile([P, 2, 512], U8, name="y_s", align_bytes=64),
+            )
+        st = {}
+
+        def copy(eng, out, in_):
+            if eng == "V":
+                nc.vector.tensor_copy(out=out, in_=in_)
+            elif eng == "G":
+                nc.gpsimd.tensor_copy(out=out, in_=in_)
+            else:
+                nc.scalar.copy(out=out, in_=in_)
+
+        def turn(words, name, eng, bufs):
+            pt = bank("p" + name)
+            ptv = pt[:].rearrange("p (a u r) -> p a u r", a=2, u=2)
+            for a in (0, 1):
+                for u in (0, 1):
+                    nc.tensor.transpose(ptv[:, a, u, :], words(a, u), ident[:])
+            gr = stage.tile([P, 256, 4], BF16, name=name, align_bytes=64, bufs=bufs)
+            o = gr[:].rearrange("p r t -> p (r t)").bitcast(F32).rearrange("p (a r u) -> p a r u", a=2, u=2)
+            copy(eng, o, ptv.rearrange("p a u r -> p a r u"))
+            return gr
+
+        def quant(dst, cs, src, pat):
+            nc.vector.quantize_mx(
+                out=dst[0][:, cs].bitcast(FP8X4), scales=dst[1][:, cs], in_=src[:].rearrange(pat)
+            )
+
+        def mx(out, a, ac, b_, bc):
+            nc.tensor.matmul_mx(
+                out=out,
+                lhsT=a[0][:, ac].bitcast(FP8X4),
+                lhsT_scale=a[1][:, ac],
+                rhs=b_[0][:, bc].bitcast(FP8X4),
+                rhs_scale=b_[1][:, bc],
+                start=True,
+                stop=True,
+            )
+
+        def prep(op, b, h, eng):
+            src = ld[op, b]
+            st["g", op, b, h] = turn(lambda a, u: src[:, 2 * h + a, :].bitcast(F32)[:, u:256:2], "gr", eng, 6)
+
+        def prepq(op, b, h):
+            quant(codes[op, b], slice(256 * h, 256 * h + 256), st["g", op, b, h], "p r t -> p (r t)")
+
+        def logits(b, T):
+            l = bank("l")
+            mx(l[:], codes["q", b], slice(128 * T, 128 * T + 128), codes["k", b], slice(0, 512))
+            m = stage.tile([P, 1], F32, name="m", bufs=8)
+            nc.vector.reduce_max(m[:], l[:], axis=AX.X)
+            nm = stage.tile([P, 1], F32, name="nm", bufs=8)
+            nc.scalar.activation(nm[:], m[:], ACT.Copy, scale=-SCALE)
+            st["l", b, T] = (l, nm)
+
+        def expo(b, T):
+            l, nm = st["l", b, T]
+            e = stage.tile([P, 512], F32, name="e", align_bytes=64)
+            s = stage.tile([P, 1], F32, name="s", bufs=8)
+            nc.scalar.activation(e[:], l[:], ACT.Exp, bias=nm[:], scale=SCALE, accum_out=s[:])
+            st["e", b, T] = (e, s)
+
+        def norm(b, T):
+            e, s = st["e", b, T]
+            r = stage.tile([P, 1], F32, name="r", bufs=8)
+            nc.vector.reciprocal(r[:], s[:])
+            w1 = stage.tile([P, 512], F32, name="w1", align_bytes=64)
+            nc.vector.tensor_scalar(w1[:], e[:], r[:], -1.0 / S, op0=ALU.mult, op1=ALU.add)
+            st["w", b, T] = w1
+
+        def shape(b, T):
+            a = stage.tile([P, 512], BF16, name="a", align_bytes=64)
+            nc.vector.tensor_tensor(
+                a[:].rearrange("i (u p e) -> i u p e", u=2, e=2),
+                st["w", b, T][:].rearrange("i (u e p) -> i u p e", u=2, e=2),
+                gb[:].rearrange("i (p u e) -> i u p e", u=2, e=2),
+                op=ALU.mult,
+            )
+            st["a", b, T] = a
+
+        def aturn(b, h, eng):
+            st["ga", b, h] = turn(
+                lambda a, u: st["a", b, 2 * h + a][:].bitcast(F32)[:, 128 * u : 128 * u + 128], "ga", eng, 4
+            )
+
+        def aquant(b, h):
+            quant(codes["a", b], slice(256 * h, 256 * h + 256), st["ga", b, h], "p r t -> p (r t)")
+
+        def value(b, c, eng):
+            if ("gv", b, c // 4) not in st:
+                st["gv", b, c // 4] = stage.tile([P, 512, 4], BF16, name="gv", align_bytes=64)
+            gr = st["gv", b, c // 4]
+            pv = bank("pv")
+            pvv = pv[:].rearrange("p (t e) -> p t e", t=4)
+            for t in range(4):
+                mx(pvv[:, t, :], codes["x", b], slice(128 * t, 128 * t + 128), (w_c, w_sc), slice(128 * c, 128 * c + 128))
+            copy(
+                eng,
+                gr[:].rearrange("p (te n) t -> p te n t", te=4)[:, :, 32 * (c % 4) : 32 * (c % 4) + 32, :],
+                pv[:].rearrange("p (t n te) -> p te n t", t=4, te=4),
+            )
+
+        def vquant(b, j):
+            quant(codes["v", b], slice(512 * j, 512 * j + 512), st["gv", b, j], "p e t -> p (e t)")
+
+        def v0turn(b, gg, u, eng):
+            pt = bank("p0")
+            ptv = pt[:].rearrange("p (a r) -> p a r", a=4)
+            for T in range(4):
+                words = ld["v", b][:, T, :].bitcast(F32)
+                nc.tensor.transpose(ptv[:, T, :], words[:, 256 * gg + u : 256 * gg + 256 : 2], ident[:])
+            v0t = stage.tile([P, 512], F32, name="v0t", align_bytes=64, bufs=8)
+            copy(eng, v0t[:], pt[:])
+            st["v0", b, gg, u] = v0t
+
+        def attend(b, gg, t):
+            if ("RT", b, gg) not in st:
+                st["RT", b, gg] = two.tile([P, 4, 512], F32, name="RT%d" % gg, align_bytes=64)
+            po = bank("po")
+            c0 = 512 * gg + 128 * t
+            mx(po[:], codes["v", b], slice(c0, c0 + 128), codes["a", b], slice(0, 512))
+            nc.vector.scalar_tensor_tensor(
+                st["RT", b, gg][:, t, :],
+                po[:],
+                beta_c[:, gg, t : t + 1],
+                st["v0", b, gg, t // 2][:].bitcast(BF16)[:, t % 2 : 1024 : 2],
+                op0=ALU.mult,
+                op1=ALU.add,
+            )
+
+        def cast(b, gg, f, eng):
+            gy = stage.tile([P, 256, 4], BF16, name="gy", align_bytes=64)
+            copy(eng, gy[:], st["RT", b, gg][:, :, 256 * f : 256 * f + 256].rearrange("p t i -> p i t"))
+            st["gy", b, gg, f] = gy
+
+        def yquant(b, gg, f):
+            yc, ys = codes["y", b]
+            cs = slice(256 * f, 256 * f + 256)
+            nc.vector.quantize_mx(
+                out=yc[:, gg, cs].bitcast(FP8X4), scales=ys[:, gg, cs], in_=st["gy", b, gg, f][:].rearrange("p r t -> p (r t)")
+            )
+            m0 = 512 * b + 256 * f
+            nc.sync.dma_start(
+                out=out_1[gg, :, m0 : m0 + 256, :].rearrange("p m t -> p (m t)").bitcast(I32),
+                in_=yc[:, gg, cs].bitcast(I32),
+            )
+            st["ny", b] = st.get(("ny", b), 0) + 1
+            if st["ny", b] == 4:
+                for Q in range(4):
+                    nc.sync.dma_start(
+                        out=out_2[:, 4 * Q : 4 * Q + 4, 512 * b : 512 * b + 512].rearrange("g q m -> q g m").bitcast(I32),
+                        in_=ys[32 * Q : 32 * Q + 4, :, :].bitcast(I32),
+                    )
+
+        def rout(b, gg, T, eng):
+            pr = bank("pr")
+            prv = pr[:].rearrange("i (t p) -> i t p", t=4)
+            for t in range(4):
+                nc.tensor.transpose(prv[:, t, :], st["RT", b, gg][:, t, 128 * T : 128 * T + 128], ident[:])
+            R = stage.tile([P, 512], F32, name="R", align_bytes=64, bufs=8)
+            copy(eng, R[:].rearrange("i (p t) -> i p t", t=4), prv.rearrange("i t p -> i p t"))
+            nc.sync.dma_start(out=out_0[b, 128 * T : 128 * T + 128, 512 * gg : 512 * gg + 512], in_=R[:])
+
+        beta_done = []
+        for f, b, i, j, eng in steps():
+            if f in ("pk", "pq", "px"):
+                prep(f[1], b, i, eng)
+            elif f in ("qk", "qq", "qx"):
+                prepq(f[1], b, i)
+            elif f == "l":
+                logits(b, i)
+            elif f == "x":
+                expo(b, i)
+            elif f == "n":
+                norm(b, i)
+            elif f == "a":
+                shape(b, i)
+            elif f == "at":
+                aturn(b, i, eng)
+            elif f == "aq":
+                aquant(b, i)
+            elif f == "vm":
+                value(b, i, eng)
+            elif f == "vq":
+                vquant(b, i)
+            elif f == "v0":
+                v0turn(b, i, j, eng)
+            elif f == "o":
+                if not beta_done:
+                    nc.vector.tensor_scalar(beta_c[:], beta_b[:], 1.0 / S, None, op0=ALU.mult)
+                    beta_done.append(1)
+                attend(b, i, j)
+            elif f == "c":
+                cast(b, i, j, eng)
+            elif f == "rq":
+                yquant(b, i, j)
+            elif f == "ro":
+                rout(b, i, j, eng)

@@ -21,41 +21,41 @@ SCALE = D ** -0.5
 
 def steps():
     return [
-        ("pk", 0, 0, 0, "S"), ("pk", 0, 1, 0, "S"), ("pq", 0, 0, 0, "S"), ("qk", 0, 0, 0, "S"),
-        ("pq", 0, 1, 0, "S"), ("qk", 0, 1, 0, "S"), ("qq", 0, 0, 0, "S"), ("qq", 0, 1, 0, "S"),
-        ("px", 0, 0, 0, "S"), ("l", 0, 0, 0, "S"), ("x", 0, 0, 0, "S"), ("l", 0, 3, 0, "S"),
-        ("l", 0, 2, 0, "S"), ("n", 0, 0, 0, "S"), ("px", 0, 1, 0, "S"), ("x", 0, 2, 0, "S"),
-        ("l", 0, 1, 0, "S"), ("qx", 0, 0, 0, "S"), ("qx", 0, 1, 0, "S"), ("x", 0, 3, 0, "S"),
-        ("n", 0, 2, 0, "S"), ("x", 0, 1, 0, "S"), ("n", 0, 3, 0, "S"), ("n", 0, 1, 0, "S"),
-        ("vm", 0, 4, 0, "S"), ("a", 0, 0, 0, "S"), ("a", 0, 2, 0, "S"), ("vm", 0, 1, 0, "S"),
-        ("vm", 0, 2, 0, "S"), ("vm", 0, 6, 0, "S"), ("vm", 0, 3, 0, "S"), ("a", 0, 1, 0, "S"),
-        ("a", 0, 3, 0, "S"), ("vm", 0, 7, 0, "S"), ("vm", 0, 5, 0, "S"), ("v0", 0, 0, 0, "V"),
-        ("vm", 0, 0, 0, "V"), ("v0", 0, 0, 1, "S"), ("at", 0, 0, 0, "V"), ("vq", 0, 0, 0, "S"),
-        ("aq", 0, 0, 0, "S"), ("at", 0, 1, 0, "S"), ("px", 1, 1, 0, "S"), ("aq", 0, 1, 0, "S"),
-        ("pq", 1, 1, 0, "S"), ("v0", 0, 1, 0, "S"), ("v0", 0, 1, 1, "S"), ("vq", 0, 1, 0, "S"),
-        ("o", 0, 0, 2, "S"), ("o", 0, 0, 1, "S"), ("o", 0, 1, 3, "S"), ("o", 0, 0, 0, "S"),
-        ("o", 0, 1, 1, "S"), ("o", 0, 0, 3, "S"), ("pq", 1, 0, 0, "S"), ("pk", 1, 1, 0, "S"),
-        ("o", 0, 1, 0, "S"), ("pk", 1, 0, 0, "S"), ("ro", 0, 0, 3, "S"), ("qq", 1, 0, 0, "S"),
-        ("qk", 1, 0, 0, "S"), ("o", 0, 1, 2, "S"), ("ro", 0, 0, 1, "S"), ("qq", 1, 1, 0, "S"),
-        ("ro", 0, 0, 0, "S"), ("px", 1, 0, 0, "S"), ("ro", 0, 1, 0, "S"), ("qk", 1, 1, 0, "S"),
-        ("qx", 1, 1, 0, "S"), ("c", 0, 0, 0, "V"), ("ro", 0, 1, 3, "S"), ("l", 1, 0, 0, "S"),
-        ("l", 1, 2, 0, "S"), ("ro", 0, 0, 2, "S"), ("x", 1, 2, 0, "S"), ("l", 1, 1, 0, "S"),
-        ("l", 1, 3, 0, "S"), ("c", 0, 1, 1, "V"), ("x", 1, 0, 0, "S"), ("n", 1, 2, 0, "S"),
-        ("x", 1, 1, 0, "S"), ("qx", 1, 0, 0, "S"), ("c", 0, 1, 0, "V"), ("x", 1, 3, 0, "S"),
-        ("vm", 1, 5, 0, "S"), ("rq", 0, 1, 1, "S"), ("n", 1, 1, 0, "S"), ("a", 1, 2, 0, "S"),
-        ("n", 1, 0, 0, "S"), ("vm", 1, 2, 0, "S"), ("ro", 0, 1, 2, "S"), ("a", 1, 1, 0, "S"),
-        ("n", 1, 3, 0, "S"), ("a", 1, 0, 0, "S"), ("vm", 1, 3, 0, "S"), ("rq", 0, 1, 0, "S"),
-        ("a", 1, 3, 0, "S"), ("vm", 1, 1, 0, "S"), ("v0", 1, 0, 1, "S"), ("vm", 1, 6, 0, "S"),
-        ("c", 0, 0, 1, "V"), ("rq", 0, 0, 0, "S"), ("vm", 1, 0, 0, "S"), ("at", 1, 0, 0, "S"),
-        ("rq", 0, 0, 1, "S"), ("vm", 1, 7, 0, "S"), ("at", 1, 1, 0, "S"), ("aq", 1, 0, 0, "S"),
-        ("vq", 1, 0, 0, "S"), ("aq", 1, 1, 0, "S"), ("vm", 1, 4, 0, "S"), ("v0", 1, 0, 0, "S"),
-        ("v0", 1, 1, 0, "S"), ("vq", 1, 1, 0, "S"), ("ro", 0, 1, 1, "S"), ("o", 1, 0, 2, "S"),
-        ("o", 1, 0, 1, "S"), ("o", 1, 0, 0, "S"), ("o", 1, 0, 3, "S"), ("v0", 1, 1, 1, "S"),
-        ("o", 1, 1, 3, "S"), ("o", 1, 1, 2, "S"), ("o", 1, 1, 0, "S"), ("ro", 1, 0, 0, "S"),
-        ("ro", 1, 0, 2, "S"), ("o", 1, 1, 1, "S"), ("c", 1, 1, 0, "V"), ("ro", 1, 0, 3, "S"),
-        ("ro", 1, 0, 1, "S"), ("c", 1, 0, 0, "V"), ("ro", 1, 1, 2, "S"), ("ro", 1, 1, 3, "S"),
-        ("ro", 1, 1, 1, "S"), ("c", 1, 0, 1, "V"), ("rq", 1, 1, 0, "S"), ("rq", 1, 0, 1, "S"),
-        ("c", 1, 1, 1, "V"), ("rq", 1, 1, 1, "S"), ("ro", 1, 1, 0, "S"), ("rq", 1, 0, 0, "S"),
+        ("pk", 0, 0, 0, "S"), ("pk", 0, 1, 0, "S"), ("qk", 0, 1, 0, "S"), ("pq", 0, 0, 0, "S"),
+        ("pq", 0, 1, 0, "S"), ("qq", 0, 0, 0, "S"), ("px", 0, 0, 0, "S"), ("qk", 0, 0, 0, "S"),
+        ("qq", 0, 1, 0, "S"), ("px", 0, 1, 0, "V"), ("l", 0, 1, 0, "S"), ("l", 0, 0, 0, "S"),
+        ("x", 0, 1, 0, "S"), ("x", 0, 0, 0, "S"), ("qx", 0, 1, 0, "S"), ("l", 0, 3, 0, "S"),
+        ("pk", 1, 1, 0, "V"), ("pq", 1, 0, 0, "S"), ("x", 0, 3, 0, "S"), ("n", 0, 1, 0, "G"),
+        ("qx", 0, 0, 0, "S"), ("pk", 1, 0, 0, "V"), ("vm", 0, 0, 0, "S"), ("qq", 1, 0, 0, "S"),
+        ("l", 0, 2, 0, "S"), ("pq", 1, 1, 0, "V"), ("qk", 1, 1, 0, "S"), ("qk", 1, 0, 0, "S"),
+        ("vm", 0, 3, 0, "S"), ("x", 0, 2, 0, "S"), ("a", 0, 1, 0, "G"), ("n", 0, 0, 0, "G"),
+        ("qq", 1, 1, 0, "S"), ("vm", 0, 2, 0, "S"), ("v0", 0, 1, 1, "S"), ("n", 0, 3, 0, "G"),
+        ("n", 0, 2, 0, "G"), ("v0", 0, 1, 0, "S"), ("l", 1, 3, 0, "S"), ("a", 0, 0, 0, "G"),
+        ("x", 1, 3, 0, "S"), ("l", 1, 1, 0, "S"), ("l", 1, 2, 0, "S"), ("vm", 0, 4, 0, "S"),
+        ("a", 0, 2, 0, "G"), ("x", 1, 1, 0, "S"), ("v0", 1, 0, 1, "V"), ("a", 0, 3, 0, "G"),
+        ("l", 1, 0, 0, "S"), ("vm", 0, 6, 0, "S"), ("vm", 0, 7, 0, "V"), ("at", 0, 0, 0, "V"),
+        ("px", 1, 0, 0, "V"), ("vm", 0, 1, 0, "S"), ("v0", 0, 0, 1, "S"), ("n", 1, 1, 0, "G"),
+        ("aq", 0, 0, 0, "S"), ("vm", 0, 5, 0, "V"), ("vq", 0, 0, 0, "S"), ("at", 0, 1, 0, "S"),
+        ("aq", 0, 1, 0, "S"), ("qx", 1, 0, 0, "S"), ("px", 1, 1, 0, "S"), ("v0", 0, 0, 0, "S"),
+        ("x", 1, 2, 0, "S"), ("qx", 1, 1, 0, "S"), ("vq", 0, 1, 0, "S"), ("a", 1, 1, 0, "G"),
+        ("o", 0, 0, 0, "S"), ("n", 1, 3, 0, "G"), ("o", 0, 0, 1, "S"), ("vm", 1, 0, 0, "S"),
+        ("x", 1, 0, 0, "S"), ("a", 1, 3, 0, "G"), ("o", 0, 1, 0, "S"), ("vm", 1, 6, 0, "S"),
+        ("n", 1, 0, 0, "S"), ("n", 1, 2, 0, "G"), ("o", 0, 0, 3, "S"), ("o", 0, 0, 2, "S"),
+        ("o", 0, 1, 3, "S"), ("vm", 1, 5, 0, "S"), ("vm", 1, 1, 0, "S"), ("o", 0, 1, 1, "S"),
+        ("v0", 1, 1, 1, "S"), ("c", 0, 0, 0, "S"), ("o", 0, 1, 2, "S"), ("ro", 0, 0, 0, "V"),
+        ("vm", 1, 3, 0, "V"), ("a", 1, 0, 0, "G"), ("a", 1, 2, 0, "G"), ("ro", 0, 0, 2, "V"),
+        ("at", 1, 0, 0, "S"), ("vm", 1, 2, 0, "S"), ("vq", 1, 0, 0, "S"), ("rq", 0, 0, 0, "S"),
+        ("aq", 1, 0, 0, "S"), ("c", 0, 1, 0, "G"), ("rq", 0, 1, 0, "S"), ("v0", 1, 0, 0, "S"),
+        ("at", 1, 1, 0, "S"), ("vm", 1, 4, 0, "S"), ("aq", 1, 1, 0, "S"), ("ro", 0, 1, 2, "S"),
+        ("ro", 0, 1, 0, "S"), ("vm", 1, 7, 0, "S"), ("c", 0, 0, 1, "G"), ("c", 0, 1, 1, "G"),
+        ("ro", 0, 0, 1, "S"), ("ro", 0, 1, 1, "S"), ("o", 1, 0, 3, "S"), ("o", 1, 0, 0, "S"),
+        ("o", 1, 0, 2, "S"), ("vq", 1, 1, 0, "S"), ("ro", 0, 0, 3, "S"), ("rq", 0, 0, 1, "S"),
+        ("ro", 0, 1, 3, "S"), ("o", 1, 0, 1, "S"), ("v0", 1, 1, 0, "S"), ("rq", 0, 1, 1, "S"),
+        ("o", 1, 1, 1, "S"), ("o", 1, 1, 3, "S"), ("ro", 1, 0, 0, "S"), ("ro", 1, 0, 2, "S"),
+        ("ro", 1, 0, 3, "S"), ("o", 1, 1, 0, "S"), ("c", 1, 0, 1, "G"), ("c", 1, 0, 0, "G"),
+        ("o", 1, 1, 2, "S"), ("ro", 1, 0, 1, "S"), ("rq", 1, 0, 1, "S"), ("rq", 1, 0, 0, "S"),
+        ("c", 1, 1, 0, "S"), ("ro", 1, 1, 2, "V"), ("ro", 1, 1, 0, "S"), ("c", 1, 1, 1, "S"),
+        ("ro", 1, 1, 3, "V"), ("rq", 1, 1, 0, "S"), ("ro", 1, 1, 1, "V"), ("rq", 1, 1, 1, "S"),
     ]
 
 
@@ -77,6 +77,8 @@ def tile_shapedcenteredattentionvalueskip_x2_kernel(
         nc.vector.memset(rows[:], 0.0)
         ones = keep.tile([P, P], BF16, align_bytes=64)
         nc.vector.memset(ones[:], 1.0)
+        minus = keep.tile([P, 1], F32)
+        nc.vector.memset(minus[:], -1.0 / S)
         warm = keep.tile([P, 1], F32)
         nc.vector.memset(warm[:], 0.0)
         nc.scalar.activation(warm[:], warm[:], ACT.Exp)
@@ -136,7 +138,7 @@ def tile_shapedcenteredattentionvalueskip_x2_kernel(
             if eng == "V":
                 nc.vector.tensor_copy(out=out, in_=in_)
             elif eng == "G":
-                nc.gpsimd.tensor_copy(out=out, in_=in_)
+                nc.gpsimd.tensor_scalar(out, in_, 1.0, 1.0, op0=ALU.mult, op1=ALU.mult)
             else:
                 nc.scalar.copy(out=out, in_=in_)
 
@@ -190,17 +192,22 @@ def tile_shapedcenteredattentionvalueskip_x2_kernel(
             nc.scalar.activation(e[:], l[:], ACT.Exp, bias=nm[:], scale=SCALE, accum_out=s[:])
             st["e", b, T] = (e, s)
 
-        def norm(b, T):
+        def norm(b, T, eng):
             e, s = st["e", b, T]
             r = stage.tile([P, 1], F32, name="r", bufs=8)
             nc.vector.reciprocal(r[:], s[:])
             w1 = stage.tile([P, 512], F32, name="w1", align_bytes=64)
-            nc.vector.tensor_scalar(w1[:], e[:], r[:], -1.0 / S, op0=ALU.mult, op1=ALU.add)
+            if eng == "S":
+                nc.scalar.activation(w1[:], e[:], ACT.Identity, bias=minus[:], scale=r[:])
+            else:
+                (nc.gpsimd if eng == "G" else nc.vector).tensor_scalar(
+                    w1[:], e[:], r[:], -1.0 / S, op0=ALU.mult, op1=ALU.add
+                )
             st["w", b, T] = w1
 
-        def shape(b, T):
+        def shape(b, T, eng):
             a = stage.tile([P, 512], BF16, name="a", align_bytes=64)
-            nc.vector.tensor_tensor(
+            (nc.gpsimd if eng == "G" else nc.vector).tensor_tensor(
                 a[:].rearrange("i (u p e) -> i u p e", u=2, e=2),
                 st["w", b, T][:].rearrange("i (u e p) -> i u p e", u=2, e=2),
                 gb[:].rearrange("i (p u e) -> i u p e", u=2, e=2),
@@ -302,9 +309,9 @@ def tile_shapedcenteredattentionvalueskip_x2_kernel(
             elif f == "x":
                 expo(b, i)
             elif f == "n":
-                norm(b, i)
+                norm(b, i, eng)
             elif f == "a":
-                shape(b, i)
+                shape(b, i, eng)
             elif f == "at":
                 aturn(b, i, eng)
             elif f == "aq":

@@ -21,41 +21,43 @@ SCALE = D ** -0.5
 
 def steps():
     return [
-        ("pk", 0, 0, 0, "S"), ("pk", 0, 1, 0, "S"), ("qk", 0, 1, 0, "S"), ("pq", 0, 0, 0, "S"),
-        ("pq", 0, 1, 0, "S"), ("qq", 0, 0, 0, "S"), ("px", 0, 0, 0, "S"), ("qk", 0, 0, 0, "S"),
-        ("qq", 0, 1, 0, "S"), ("px", 0, 1, 0, "V"), ("l", 0, 1, 0, "S"), ("l", 0, 0, 0, "S"),
-        ("x", 0, 1, 0, "S"), ("x", 0, 0, 0, "S"), ("qx", 0, 1, 0, "S"), ("l", 0, 3, 0, "S"),
-        ("pk", 1, 1, 0, "V"), ("pq", 1, 0, 0, "S"), ("x", 0, 3, 0, "S"), ("n", 0, 1, 0, "G"),
-        ("qx", 0, 0, 0, "S"), ("pk", 1, 0, 0, "V"), ("vm", 0, 0, 0, "S"), ("qq", 1, 0, 0, "S"),
-        ("l", 0, 2, 0, "S"), ("pq", 1, 1, 0, "V"), ("qk", 1, 1, 0, "S"), ("qk", 1, 0, 0, "S"),
-        ("vm", 0, 3, 0, "S"), ("x", 0, 2, 0, "S"), ("a", 0, 1, 0, "G"), ("n", 0, 0, 0, "G"),
-        ("qq", 1, 1, 0, "S"), ("vm", 0, 2, 0, "S"), ("v0", 0, 1, 1, "S"), ("n", 0, 3, 0, "G"),
-        ("n", 0, 2, 0, "G"), ("v0", 0, 1, 0, "S"), ("l", 1, 3, 0, "S"), ("a", 0, 0, 0, "G"),
-        ("x", 1, 3, 0, "S"), ("l", 1, 1, 0, "S"), ("l", 1, 2, 0, "S"), ("vm", 0, 4, 0, "S"),
-        ("a", 0, 2, 0, "G"), ("x", 1, 1, 0, "S"), ("v0", 1, 0, 1, "V"), ("a", 0, 3, 0, "G"),
-        ("l", 1, 0, 0, "S"), ("vm", 0, 6, 0, "S"), ("vm", 0, 7, 0, "V"), ("at", 0, 0, 0, "V"),
-        ("px", 1, 0, 0, "V"), ("vm", 0, 1, 0, "S"), ("v0", 0, 0, 1, "S"), ("n", 1, 1, 0, "G"),
-        ("aq", 0, 0, 0, "S"), ("vm", 0, 5, 0, "V"), ("vq", 0, 0, 0, "S"), ("at", 0, 1, 0, "S"),
-        ("aq", 0, 1, 0, "S"), ("qx", 1, 0, 0, "S"), ("px", 1, 1, 0, "S"), ("v0", 0, 0, 0, "S"),
-        ("x", 1, 2, 0, "S"), ("qx", 1, 1, 0, "S"), ("vq", 0, 1, 0, "S"), ("a", 1, 1, 0, "G"),
-        ("o", 0, 0, 0, "S"), ("n", 1, 3, 0, "G"), ("o", 0, 0, 1, "S"), ("vm", 1, 0, 0, "S"),
-        ("x", 1, 0, 0, "S"), ("a", 1, 3, 0, "G"), ("o", 0, 1, 0, "S"), ("vm", 1, 6, 0, "S"),
-        ("n", 1, 0, 0, "S"), ("n", 1, 2, 0, "G"), ("o", 0, 0, 3, "S"), ("o", 0, 0, 2, "S"),
-        ("o", 0, 1, 3, "S"), ("vm", 1, 5, 0, "S"), ("vm", 1, 1, 0, "S"), ("o", 0, 1, 1, "S"),
-        ("v0", 1, 1, 1, "S"), ("c", 0, 0, 0, "S"), ("o", 0, 1, 2, "S"), ("ro", 0, 0, 0, "V"),
-        ("vm", 1, 3, 0, "V"), ("a", 1, 0, 0, "G"), ("a", 1, 2, 0, "G"), ("ro", 0, 0, 2, "V"),
-        ("at", 1, 0, 0, "S"), ("vm", 1, 2, 0, "S"), ("vq", 1, 0, 0, "S"), ("rq", 0, 0, 0, "S"),
-        ("aq", 1, 0, 0, "S"), ("c", 0, 1, 0, "G"), ("rq", 0, 1, 0, "S"), ("v0", 1, 0, 0, "S"),
-        ("at", 1, 1, 0, "S"), ("vm", 1, 4, 0, "S"), ("aq", 1, 1, 0, "S"), ("ro", 0, 1, 2, "S"),
-        ("ro", 0, 1, 0, "S"), ("vm", 1, 7, 0, "S"), ("c", 0, 0, 1, "G"), ("c", 0, 1, 1, "G"),
-        ("ro", 0, 0, 1, "S"), ("ro", 0, 1, 1, "S"), ("o", 1, 0, 3, "S"), ("o", 1, 0, 0, "S"),
-        ("o", 1, 0, 2, "S"), ("vq", 1, 1, 0, "S"), ("ro", 0, 0, 3, "S"), ("rq", 0, 0, 1, "S"),
-        ("ro", 0, 1, 3, "S"), ("o", 1, 0, 1, "S"), ("v0", 1, 1, 0, "S"), ("rq", 0, 1, 1, "S"),
-        ("o", 1, 1, 1, "S"), ("o", 1, 1, 3, "S"), ("ro", 1, 0, 0, "S"), ("ro", 1, 0, 2, "S"),
-        ("ro", 1, 0, 3, "S"), ("o", 1, 1, 0, "S"), ("c", 1, 0, 1, "G"), ("c", 1, 0, 0, "G"),
-        ("o", 1, 1, 2, "S"), ("ro", 1, 0, 1, "S"), ("rq", 1, 0, 1, "S"), ("rq", 1, 0, 0, "S"),
-        ("c", 1, 1, 0, "S"), ("ro", 1, 1, 2, "V"), ("ro", 1, 1, 0, "S"), ("c", 1, 1, 1, "S"),
-        ("ro", 1, 1, 3, "V"), ("rq", 1, 1, 0, "S"), ("ro", 1, 1, 1, "V"), ("rq", 1, 1, 1, "S"),
+        ("pk", 0, 0, 0, "V"), ("pk", 0, 1, 0, "S"), ("qk", 0, 0, 0, "S"), ("pq", 0, 0, 0, "S"),
+        ("qq", 0, 0, 0, "S"), ("pq", 0, 1, 0, "S"), ("qk", 0, 1, 0, "S"), ("qq", 0, 1, 0, "S"),
+        ("px", 0, 0, 0, "S"), ("qx", 0, 0, 0, "S"), ("px", 0, 1, 0, "S"), ("l", 0, 0, 0, "S"),
+        ("pk", 1, 0, 0, "S"), ("qx", 0, 1, 0, "S"), ("x", 0, 0, 0, "S"), ("l", 0, 1, 0, "S"),
+        ("x", 0, 1, 0, "S"), ("qk", 1, 0, 0, "S"), ("n", 0, 0, 0, "G"), ("l", 0, 2, 0, "S"),
+        ("a", 0, 0, 0, "G"), ("pk", 1, 1, 0, "V"), ("pq", 1, 0, 0, "S"), ("vm", 0, 0, 0, "V"),
+        ("x", 0, 2, 0, "S"), ("n", 0, 1, 0, "G"), ("vm", 0, 1, 0, "S"), ("l", 0, 3, 0, "S"),
+        ("vm", 0, 2, 0, "V"), ("x", 0, 3, 0, "S"), ("pq", 1, 1, 0, "V"), ("n", 0, 2, 0, "S"),
+        ("qk", 1, 1, 0, "S"), ("px", 1, 0, 0, "S"), ("qq", 1, 0, 0, "S"), ("n", 0, 3, 0, "S"),
+        ("vm", 0, 3, 0, "V"), ("a", 0, 1, 0, "V"), ("px", 1, 1, 0, "S"), ("a", 0, 2, 0, "V"),
+        ("qx", 1, 0, 0, "S"), ("vm", 0, 4, 0, "S"), ("vm", 0, 5, 0, "S"), ("l", 1, 0, 0, "S"),
+        ("vm", 0, 6, 0, "V"), ("vm", 0, 7, 0, "S"), ("x", 1, 0, 0, "S"), ("l", 1, 1, 0, "S"),
+        ("qq", 1, 1, 0, "S"), ("vq", 0, 0, 0, "S"), ("a", 0, 3, 0, "G"), ("qx", 1, 1, 0, "S"),
+        ("at", 0, 0, 0, "S"), ("n", 1, 0, 0, "S"), ("at", 0, 1, 0, "S"), ("x", 1, 1, 0, "S"),
+        ("vq", 0, 1, 0, "S"), ("aq", 0, 0, 0, "S"), ("l", 1, 2, 0, "S"), ("a", 1, 0, 0, "G"),
+        ("x", 1, 2, 0, "S"), ("l", 1, 3, 0, "S"), ("vm", 1, 0, 0, "S"), ("o", 0, 0, 0, "S"),
+        ("vm", 1, 1, 0, "S"), ("aq", 0, 1, 0, "S"), ("n", 1, 1, 0, "S"), ("x", 1, 3, 0, "S"),
+        ("ad", 0, 0, 0, "G"), ("o", 0, 0, 1, "S"), ("o", 0, 1, 0, "S"), ("o", 0, 1, 1, "S"),
+        ("o", 0, 2, 0, "S"), ("ad", 0, 0, 1, "G"), ("n", 1, 2, 0, "S"), ("vm", 1, 2, 0, "S"),
+        ("o", 0, 2, 1, "S"), ("vm", 1, 3, 0, "S"), ("o", 0, 3, 0, "S"), ("o", 0, 3, 1, "S"),
+        ("n", 1, 3, 0, "S"), ("a", 1, 1, 0, "V"), ("vm", 1, 4, 0, "S"), ("ad", 0, 1, 0, "G"),
+        ("c", 0, 0, 0, "V"), ("at", 1, 0, 0, "S"), ("ad", 0, 1, 1, "V"), ("vm", 1, 5, 0, "S"),
+        ("vm", 1, 6, 0, "S"), ("vm", 1, 7, 0, "S"), ("ad", 0, 2, 0, "V"), ("vq", 1, 0, 0, "S"),
+        ("c", 0, 0, 1, "S"), ("a", 1, 2, 0, "V"), ("aq", 1, 0, 0, "S"), ("a", 1, 3, 0, "V"),
+        ("c", 0, 1, 0, "S"), ("ad", 0, 2, 1, "V"), ("at", 1, 1, 0, "S"), ("vq", 1, 1, 0, "S"),
+        ("ad", 0, 3, 0, "V"), ("o", 1, 0, 0, "S"), ("o", 1, 0, 1, "S"), ("ad", 0, 3, 1, "G"),
+        ("o", 1, 1, 0, "S"), ("aq", 1, 1, 0, "S"), ("c", 0, 1, 1, "S"), ("c", 0, 2, 0, "S"),
+        ("ad", 1, 0, 0, "V"), ("ad", 1, 0, 1, "V"), ("o", 1, 1, 1, "S"), ("c", 0, 2, 1, "S"),
+        ("c", 0, 3, 0, "S"), ("rt", 0, 0, 0, "S"), ("c", 1, 0, 0, "S"), ("rt", 0, 0, 1, "S"),
+        ("ad", 1, 1, 0, "G"), ("c", 1, 0, 1, "S"), ("c", 0, 3, 1, "S"), ("o", 1, 2, 0, "S"),
+        ("o", 1, 2, 1, "S"), ("c", 1, 1, 0, "S"), ("ad", 1, 1, 1, "G"), ("o", 1, 3, 0, "S"),
+        ("o", 1, 3, 1, "S"), ("ad", 1, 2, 0, "V"), ("rt", 0, 1, 0, "S"), ("c", 1, 1, 1, "S"),
+        ("c", 1, 2, 0, "S"), ("rt", 1, 0, 0, "S"), ("ad", 1, 2, 1, "V"), ("ad", 1, 3, 0, "V"),
+        ("ad", 1, 3, 1, "V"), ("c", 1, 2, 1, "V"), ("rq", 0, 0, 0, "S"), ("c", 1, 3, 0, "S"),
+        ("rt", 0, 1, 1, "S"), ("c", 1, 3, 1, "V"), ("rq", 0, 0, 1, "S"), ("rq", 0, 1, 0, "S"),
+        ("rq", 0, 1, 1, "S"), ("rt", 1, 0, 1, "S"), ("rt", 1, 1, 0, "S"), ("rt", 1, 1, 1, "S"),
+        ("rq", 1, 0, 0, "S"), ("rq", 1, 0, 1, "S"), ("rq", 1, 1, 0, "S"), ("rq", 1, 1, 1, "S"),
     ]
 
 
@@ -73,8 +75,10 @@ def tile_shapedcenteredattentionvalueskip_x2_kernel(
         def bank(name):
             return psum.tile([P, 512], F32, name=name, tag="bank")
 
-        rows = keep.tile([P, S], BF16, align_bytes=64)
+        rows = keep.tile([P, S + E], BF16, align_bytes=64)
         nc.vector.memset(rows[:], 0.0)
+        zeros = keep.tile([P, 512], BF16, align_bytes=64)
+        nc.vector.memset(zeros[:], 0.0)
         ones = keep.tile([P, P], BF16, align_bytes=64)
         nc.vector.memset(ones[:], 1.0)
         minus = keep.tile([P, 1], F32)
@@ -88,8 +92,7 @@ def tile_shapedcenteredattentionvalueskip_x2_kernel(
         make_identity(nc, ident[:])
 
         w_c = keep.tile([P, E], U32, align_bytes=64)
-        beta_b = keep.tile([P, 2, 4], BF16)
-        beta_c = keep.tile([P, 2, 4], F32)
+        bb = keep.tile([P, E], F32, align_bytes=64)
         gb = keep.tile([P, S], F32, align_bytes=64)
         ld = {}
         for b in range(B):
@@ -103,7 +106,8 @@ def tile_shapedcenteredattentionvalueskip_x2_kernel(
                 out=ld[op, b][:, 2 * h : 2 * h + 2, :], in_=src[b].rearrange(order, t=4)[:, 2 * h : 2 * h + 2, :]
             )
 
-        nc.scalar.dma_start(out=rows[0:1, :], in_=g.rearrange("(o s) -> o s", o=1))
+        nc.scalar.dma_start(out=rows[0:1, 0:S], in_=g.rearrange("(o s) -> o s", o=1))
+        nc.scalar.dma_start(out=rows[0:1, S : S + E], in_=beta.rearrange("(o s) -> o s", o=1))
         for op, src in (("k", k), ("q", q), ("x", x)):
             for h in (0, 1):
                 load(op, src, 0, h)
@@ -112,14 +116,20 @@ def tile_shapedcenteredattentionvalueskip_x2_kernel(
                 out=w_sc[32 * Q : 32 * Q + 4, :].bitcast(I32), in_=w_scales[0, 4 * Q : 4 * Q + 4, :].bitcast(I32)
             )
         nc.sync.dma_start(out=w_c[:].bitcast(I32), in_=w_words[0].rearrange("p n t -> p (n t)").bitcast(I32))
-        nc.sync.dma_start(out=beta_b[:], in_=beta.rearrange("(g p t) -> p g t", g=2, t=4))
         for op, src, b in (("k", k, 1), ("q", q, 1), ("v", v0, 0), ("x", x, 1), ("v", v0, 1)):
             for h in (0, 1):
                 load(op, src, b, h)
 
-        pg = bank("pg")
-        nc.tensor.matmul(pg[:], lhsT=ones[:], rhs=rows[:], start=True, stop=True)
-        nc.scalar.activation(gb[:], pg[:], ACT.Copy, scale=float(S))
+        pd = bank("pd")
+        for n in range(9):
+            nc.tensor.matmul(pd[:], lhsT=ones[:], rhs=zeros[:], start=True, stop=True)
+        for c in range(3):
+            pg = bank("pg")
+            nc.tensor.matmul(pg[:], lhsT=ones[:], rhs=rows[:, 512 * c : 512 * c + 512], start=True, stop=True)
+            if c == 0:
+                nc.scalar.activation(gb[:], pg[:], ACT.Copy, scale=float(S))
+            else:
+                nc.scalar.activation(bb[:, 512 * (c - 1) : 512 * c], pg[:], ACT.Copy, scale=1.0 / S)
 
         codes = {}
         for b in range(B):
@@ -231,55 +241,50 @@ def tile_shapedcenteredattentionvalueskip_x2_kernel(
             pvv = pv[:].rearrange("p (t e) -> p t e", t=4)
             for t in range(4):
                 mx(pvv[:, t, :], codes["x", b], slice(128 * t, 128 * t + 128), (w_c, w_sc), slice(128 * c, 128 * c + 128))
-            copy(
-                eng,
-                gr[:].rearrange("p (te n) t -> p te n t", te=4)[:, :, 32 * (c % 4) : 32 * (c % 4) + 32, :],
-                pv[:].rearrange("p (t n te) -> p te n t", t=4, te=4),
-            )
+            copy(eng, gr[:, 128 * (c % 4) : 128 * (c % 4) + 128, :], pvv.rearrange("p t e -> p e t"))
 
         def vquant(b, j):
             quant(codes["v", b], slice(512 * j, 512 * j + 512), st["gv", b, j], "p e t -> p (e t)")
 
-        def v0turn(b, gg, u, eng):
-            pt = bank("p0")
-            ptv = pt[:].rearrange("p (a r) -> p a r", a=4)
-            for T in range(4):
-                words = ld["v", b][:, T, :].bitcast(F32)
-                nc.tensor.transpose(ptv[:, T, :], words[:, 256 * gg + u : 256 * gg + 256 : 2], ident[:])
-            v0t = stage.tile([P, 512], F32, name="v0t", align_bytes=64, bufs=8)
-            copy(eng, v0t[:], pt[:])
-            st["v0", b, gg, u] = v0t
-
-        def attend(b, gg, t):
-            if ("RT", b, gg) not in st:
-                st["RT", b, gg] = two.tile([P, 4, 512], F32, name="RT%d" % gg, align_bytes=64)
+        def attend(b, T, h):
             po = bank("po")
-            c0 = 512 * gg + 128 * t
-            mx(po[:], codes["v", b], slice(c0, c0 + 128), codes["a", b], slice(0, 512))
-            nc.vector.scalar_tensor_tensor(
-                st["RT", b, gg][:, t, :],
-                po[:],
-                beta_c[:, gg, t : t + 1],
-                st["v0", b, gg, t // 2][:].bitcast(BF16)[:, t % 2 : 1024 : 2],
-                op0=ALU.mult,
-                op1=ALU.add,
+            mx(po[:], codes["a", b], slice(128 * T, 128 * T + 128), codes["v", b], slice(512 * h, 512 * h + 512))
+            t1 = stage.tile([P, 512], F32, name="t1", align_bytes=64, bufs=8)
+            nc.vector.tensor_tensor(t1[:], po[:], bb[:, 512 * h : 512 * h + 512], op=ALU.mult)
+            st["t1", b, T, h] = t1
+
+        def skip(b, T, h, eng):
+            R = stage.tile([P, 512], F32, name="R", align_bytes=64, bufs=8)
+            (nc.gpsimd if eng == "G" else nc.vector).tensor_tensor(
+                R[:], st["t1", b, T, h][:], ld["v", b][:, T, 512 * h : 512 * h + 512], op=ALU.add
+            )
+            st["R", b, T, h] = R
+            nc.sync.dma_start(out=out_0[b, 128 * T : 128 * T + 128, 512 * h : 512 * h + 512], in_=R[:])
+
+        def cast(b, T, h, eng):
+            rb = stage.tile([P, 512], BF16, name="rb", align_bytes=64, bufs=8)
+            copy(
+                eng,
+                rb[:].rearrange("i (u p e) -> i u p e", u=2, e=2),
+                st["R", b, T, h][:].rearrange("i (p u e) -> i u p e", u=2, e=2),
+            )
+            st["rb", b, T, h] = rb
+
+        def rturn(b, f, h, eng):
+            st["gy", b, f, h] = turn(
+                lambda a, u: st["rb", b, 2 * f + a, h][:].bitcast(F32)[:, 128 * u : 128 * u + 128], "gy", eng, 4
             )
 
-        def cast(b, gg, f, eng):
-            gy = stage.tile([P, 256, 4], BF16, name="gy", align_bytes=64)
-            copy(eng, gy[:], st["RT", b, gg][:, :, 256 * f : 256 * f + 256].rearrange("p t i -> p i t"))
-            st["gy", b, gg, f] = gy
-
-        def yquant(b, gg, f):
+        def yquant(b, f, h):
             yc, ys = codes["y", b]
             cs = slice(256 * f, 256 * f + 256)
             nc.vector.quantize_mx(
-                out=yc[:, gg, cs].bitcast(FP8X4), scales=ys[:, gg, cs], in_=st["gy", b, gg, f][:].rearrange("p r t -> p (r t)")
+                out=yc[:, h, cs].bitcast(FP8X4), scales=ys[:, h, cs], in_=st["gy", b, f, h][:].rearrange("p r t -> p (r t)")
             )
             m0 = 512 * b + 256 * f
             nc.sync.dma_start(
-                out=out_1[gg, :, m0 : m0 + 256, :].rearrange("p m t -> p (m t)").bitcast(I32),
-                in_=yc[:, gg, cs].bitcast(I32),
+                out=out_1[h, :, m0 : m0 + 256, :].rearrange("p m t -> p (m t)").bitcast(I32),
+                in_=yc[:, h, cs].bitcast(I32),
             )
             st["ny", b] = st.get(("ny", b), 0) + 1
             if st["ny", b] == 4:
@@ -289,16 +294,6 @@ def tile_shapedcenteredattentionvalueskip_x2_kernel(
                         in_=ys[32 * Q : 32 * Q + 4, :, :].bitcast(I32),
                     )
 
-        def rout(b, gg, T, eng):
-            pr = bank("pr")
-            prv = pr[:].rearrange("i (t p) -> i t p", t=4)
-            for t in range(4):
-                nc.tensor.transpose(prv[:, t, :], st["RT", b, gg][:, t, 128 * T : 128 * T + 128], ident[:])
-            R = stage.tile([P, 512], F32, name="R", align_bytes=64, bufs=8)
-            copy(eng, R[:].rearrange("i (p t) -> i p t", t=4), prv.rearrange("i t p -> i p t"))
-            nc.sync.dma_start(out=out_0[b, 128 * T : 128 * T + 128, 512 * gg : 512 * gg + 512], in_=R[:])
-
-        beta_done = []
         for f, b, i, j, eng in steps():
             if f in ("pk", "pq", "px"):
                 prep(f[1], b, i, eng)
@@ -320,16 +315,13 @@ def tile_shapedcenteredattentionvalueskip_x2_kernel(
                 value(b, i, eng)
             elif f == "vq":
                 vquant(b, i)
-            elif f == "v0":
-                v0turn(b, i, j, eng)
             elif f == "o":
-                if not beta_done:
-                    nc.vector.tensor_scalar(beta_c[:], beta_b[:], 1.0 / S, None, op0=ALU.mult)
-                    beta_done.append(1)
                 attend(b, i, j)
+            elif f == "ad":
+                skip(b, i, j, eng)
             elif f == "c":
                 cast(b, i, j, eng)
             elif f == "rq":
                 yquant(b, i, j)
-            elif f == "ro":
-                rout(b, i, j, eng)
+            elif f == "rt":
+                rturn(b, i, j, eng)

@@ -1,3 +1,4 @@
+import math
 from contextlib import ExitStack
 
 import concourse.mybir as mybir
@@ -15,50 +16,32 @@ AX = mybir.AxisListType
 
 B, S, D, E = 2, 512, 512, 1024
 P = 128
+HALF = 512
+ALL_TILES = B * S // P
+HALF_TILES = S // P * (E // HALF)
 FLOPS = 2 * B * S * S * D + 2 * B * S * D * E + 2 * B * S * S * E
-SCALE = D ** -0.5
 
-
-def steps():
-    return [
-        ("pk", 0, 0, 0, "V"), ("pk", 0, 1, 0, "S"), ("qk", 0, 0, 0, "S"), ("pq", 0, 0, 0, "S"),
-        ("qq", 0, 0, 0, "S"), ("pq", 0, 1, 0, "S"), ("qk", 0, 1, 0, "S"), ("qq", 0, 1, 0, "S"),
-        ("px", 0, 0, 0, "S"), ("qx", 0, 0, 0, "S"), ("px", 0, 1, 0, "S"), ("l", 0, 0, 0, "S"),
-        ("pk", 1, 0, 0, "S"), ("qx", 0, 1, 0, "S"), ("x", 0, 0, 0, "S"), ("l", 0, 1, 0, "S"),
-        ("x", 0, 1, 0, "S"), ("qk", 1, 0, 0, "S"), ("n", 0, 0, 0, "G"), ("l", 0, 2, 0, "S"),
-        ("a", 0, 0, 0, "G"), ("pk", 1, 1, 0, "V"), ("pq", 1, 0, 0, "S"), ("vm", 0, 0, 0, "V"),
-        ("x", 0, 2, 0, "S"), ("n", 0, 1, 0, "G"), ("vm", 0, 1, 0, "S"), ("l", 0, 3, 0, "S"),
-        ("vm", 0, 2, 0, "V"), ("x", 0, 3, 0, "S"), ("pq", 1, 1, 0, "V"), ("n", 0, 2, 0, "S"),
-        ("qk", 1, 1, 0, "S"), ("px", 1, 0, 0, "S"), ("qq", 1, 0, 0, "S"), ("n", 0, 3, 0, "S"),
-        ("vm", 0, 3, 0, "V"), ("a", 0, 1, 0, "V"), ("px", 1, 1, 0, "S"), ("a", 0, 2, 0, "V"),
-        ("qx", 1, 0, 0, "S"), ("vm", 0, 4, 0, "S"), ("vm", 0, 5, 0, "S"), ("l", 1, 0, 0, "S"),
-        ("vm", 0, 6, 0, "V"), ("vm", 0, 7, 0, "S"), ("x", 1, 0, 0, "S"), ("l", 1, 1, 0, "S"),
-        ("qq", 1, 1, 0, "S"), ("vq", 0, 0, 0, "S"), ("a", 0, 3, 0, "G"), ("qx", 1, 1, 0, "S"),
-        ("at", 0, 0, 0, "S"), ("n", 1, 0, 0, "S"), ("at", 0, 1, 0, "S"), ("x", 1, 1, 0, "S"),
-        ("vq", 0, 1, 0, "S"), ("aq", 0, 0, 0, "S"), ("l", 1, 2, 0, "S"), ("a", 1, 0, 0, "G"),
-        ("x", 1, 2, 0, "S"), ("l", 1, 3, 0, "S"), ("vm", 1, 0, 0, "S"), ("o", 0, 0, 0, "S"),
-        ("vm", 1, 1, 0, "S"), ("aq", 0, 1, 0, "S"), ("n", 1, 1, 0, "S"), ("x", 1, 3, 0, "S"),
-        ("ad", 0, 0, 0, "G"), ("o", 0, 0, 1, "S"), ("o", 0, 1, 0, "S"), ("o", 0, 1, 1, "S"),
-        ("o", 0, 2, 0, "S"), ("ad", 0, 0, 1, "G"), ("n", 1, 2, 0, "S"), ("vm", 1, 2, 0, "S"),
-        ("o", 0, 2, 1, "S"), ("vm", 1, 3, 0, "S"), ("o", 0, 3, 0, "S"), ("o", 0, 3, 1, "S"),
-        ("n", 1, 3, 0, "S"), ("a", 1, 1, 0, "V"), ("vm", 1, 4, 0, "S"), ("ad", 0, 1, 0, "G"),
-        ("c", 0, 0, 0, "V"), ("at", 1, 0, 0, "S"), ("ad", 0, 1, 1, "V"), ("vm", 1, 5, 0, "S"),
-        ("vm", 1, 6, 0, "S"), ("vm", 1, 7, 0, "S"), ("ad", 0, 2, 0, "V"), ("vq", 1, 0, 0, "S"),
-        ("c", 0, 0, 1, "S"), ("a", 1, 2, 0, "V"), ("aq", 1, 0, 0, "S"), ("a", 1, 3, 0, "V"),
-        ("c", 0, 1, 0, "S"), ("ad", 0, 2, 1, "V"), ("at", 1, 1, 0, "S"), ("vq", 1, 1, 0, "S"),
-        ("ad", 0, 3, 0, "V"), ("o", 1, 0, 0, "S"), ("o", 1, 0, 1, "S"), ("ad", 0, 3, 1, "G"),
-        ("o", 1, 1, 0, "S"), ("aq", 1, 1, 0, "S"), ("c", 0, 1, 1, "S"), ("c", 0, 2, 0, "S"),
-        ("ad", 1, 0, 0, "V"), ("ad", 1, 0, 1, "V"), ("o", 1, 1, 1, "S"), ("c", 0, 2, 1, "S"),
-        ("c", 0, 3, 0, "S"), ("rt", 0, 0, 0, "S"), ("c", 1, 0, 0, "S"), ("rt", 0, 0, 1, "S"),
-        ("ad", 1, 1, 0, "G"), ("c", 1, 0, 1, "S"), ("c", 0, 3, 1, "S"), ("o", 1, 2, 0, "S"),
-        ("o", 1, 2, 1, "S"), ("c", 1, 1, 0, "S"), ("ad", 1, 1, 1, "G"), ("o", 1, 3, 0, "S"),
-        ("o", 1, 3, 1, "S"), ("ad", 1, 2, 0, "V"), ("rt", 0, 1, 0, "S"), ("c", 1, 1, 1, "S"),
-        ("c", 1, 2, 0, "S"), ("rt", 1, 0, 0, "S"), ("ad", 1, 2, 1, "V"), ("ad", 1, 3, 0, "V"),
-        ("ad", 1, 3, 1, "V"), ("c", 1, 2, 1, "V"), ("rq", 0, 0, 0, "S"), ("c", 1, 3, 0, "S"),
-        ("rt", 0, 1, 1, "S"), ("c", 1, 3, 1, "V"), ("rq", 0, 0, 1, "S"), ("rq", 0, 1, 0, "S"),
-        ("rq", 0, 1, 1, "S"), ("rt", 1, 0, 1, "S"), ("rt", 1, 1, 0, "S"), ("rt", 1, 1, 1, "S"),
-        ("rq", 1, 0, 0, "S"), ("rq", 1, 0, 1, "S"), ("rq", 1, 1, 0, "S"), ("rq", 1, 1, 1, "S"),
-    ]
+ORDER = """
+    turn_k:V 0 0, turn_k:V 0 1, quant_k 0 0, turn_q 0 0, quant_k 0 1, quant_q 0 0, turn_q 0 1, turn_x 0 0,
+    turn_x 0 1, quant_q 0 1, logits 0 0, exp 0 0, logits 0 1, logits 0 2, quant_x 0 0, norm:G 0 0, exp 0 1,
+    exp 0 2, quant_x 0 1, turn_k:V 1 0, norm:G 0 1, turn_q 1 0, quant_k 1 0, spread_g, value 0 0, logits 0 3,
+    value 0 1, norm:G 0 2, value 0 2, shape 0 0, shape 0 1, quant_q 1 0, turn_x:V 1 0, value 0 3, value:V 0 4,
+    quant_x 1 0, turn_k 1 1, turn_q 1 1, quant_v 0 0, turn_x 1 1, quant_k 1 1, turn_a 0 0, exp 0 3,
+    quant_q 1 1, value 0 5, value 0 6, value 0 7, shape 0 2, quant_x 1 1, quant_a 0 0, logits 1 0, norm:G 0 3,
+    logits 1 1, attend 0 0 0, quant_v 0 1, value 1 0, exp 1 0, exp 1 1, value 1 1, shape 0 3, logits 1 2,
+    value 1 2, skip:G 0 0 0, norm:G 1 0, exp 1 2, attend 0 0 1, norm 1 1, skip:G 0 0 1, logits 1 3,
+    turn_a:V 0 1, attend 0 1 0, value 1 3, skip:G 0 1 0, quant_a 0 1, value 1 4, attend 0 1 1, exp 1 3,
+    shape 1 0, value 1 5, shape 1 1, value 1 6, attend 0 2 0, attend 0 2 1, attend 0 3 0, turn_a 1 0,
+    value 1 7, norm 1 2, norm 1 3, quant_v 1 0, quant_a 1 0, quant_v 1 1, shape 1 2, skip:G 0 1 1,
+    skip:G 0 2 0, round 0 0 0, round 0 0 1, attend 1 0 0, round 0 1 0, skip:G 0 2 1, shape 1 3, attend 0 3 1,
+    attend 1 0 1, skip:G 0 3 0, attend 1 1 0, round 0 1 1, skip:G 1 0 0, turn_a 1 1, quant_a 1 1, skip 1 0 1,
+    skip:G 1 1 0, turn_y 0 0 0, attend 1 1 1, round 0 2 0, attend 1 2 0, attend 1 2 1, attend 1 3 0,
+    round 1 0 0, round 0 2 1, round 1 0 1, attend 1 3 1, round 1 1 0, round 0 3 0, skip:G 0 3 1, skip 1 1 1,
+    round 0 3 1, skip 1 2 0, turn_y 0 0 1, round 1 1 1, skip 1 2 1, turn_y 0 1 0, turn_y 0 1 1, quant_y 0 0 0,
+    skip 1 3 0, quant_y 0 0 1, quant_y 0 1 0, quant_y 0 1 1, skip 1 3 1, round 1 2 0, round 1 2 1,
+    round:V 1 3 0, round:V 1 3 1, turn_y 1 0 0, quant_y 1 0 0, turn_y 1 0 1, turn_y:V 1 1 0, turn_y 1 1 1,
+    quant_y 1 0 1, quant_y 1 1 0, quant_y 1 1 1
+"""
 
 
 def tile_shapedcenteredattentionvalueskip_x2_kernel(
@@ -66,262 +49,257 @@ def tile_shapedcenteredattentionvalueskip_x2_kernel(
 ):
     nc = tc.nc
     with ExitStack() as ctx:
-        keep = ctx.enter_context(tc.tile_pool(name="keep", bufs=1))
-        two = ctx.enter_context(tc.tile_pool(name="two", bufs=2))
-        stage = ctx.enter_context(tc.tile_pool(name="stage", bufs=4))
-        psum = ctx.enter_context(tc.psum_pool(name="psum", bufs=8))
+        once = ctx.enter_context(tc.tile_pool(name="once", bufs=1))
+        per_batch = ctx.enter_context(tc.tile_pool(name="per_batch", bufs=B))
+        stream = ctx.enter_context(tc.tile_pool(name="stream", bufs=4))
+        psum = ctx.enter_context(tc.psum_pool(name="psum", bufs=7))
+        psum_g = ctx.enter_context(tc.psum_pool(name="psum_g", bufs=1))
         ctx.enter_context(tc.manual_schedule())
 
         def bank(name):
             return psum.tile([P, 512], F32, name=name, tag="bank")
 
-        rows = keep.tile([P, S + E], BF16, align_bytes=64)
-        nc.vector.memset(rows[:], 0.0)
-        zeros = keep.tile([P, 512], BF16, align_bytes=64)
-        nc.vector.memset(zeros[:], 0.0)
-        ones = keep.tile([P, P], BF16, align_bytes=64)
-        nc.vector.memset(ones[:], 1.0)
-        minus = keep.tile([P, 1], F32)
+        g_rows = once.tile([P, S], BF16, align_bytes=64)
+        nc.vector.memset(g_rows[:], 0.0)
+        w_scale = once.tile([P, E], U8, align_bytes=64)
+        nc.vector.memset(w_scale[:].bitcast(I32), 0)
+        one = once.tile([P, P], BF16, align_bytes=64)
+        nc.vector.memset(one[:], 1.0)
+        minus = once.tile([P, 1], F32)
         nc.vector.memset(minus[:], -1.0 / S)
-        warm = keep.tile([P, 1], F32)
-        nc.vector.memset(warm[:], 0.0)
-        nc.scalar.activation(warm[:], warm[:], ACT.Exp)
-        w_sc = keep.tile([P, E], U8, align_bytes=64)
-        nc.vector.memset(w_sc[:].bitcast(I32), 0)
-        ident = keep.tile([P, P], F32, align_bytes=64)
-        make_identity(nc, ident[:])
+        all_512 = once.tile([P, P], BF16, align_bytes=64)
+        nc.scalar.activation(all_512[:], one[:], ACT.Exp, scale=math.log(S))
+        identity = once.tile([P, P], F32, align_bytes=64)
+        make_identity(nc, identity[:])
 
-        w_c = keep.tile([P, E], U32, align_bytes=64)
-        bb = keep.tile([P, E], F32, align_bytes=64)
-        gb = keep.tile([P, S], F32, align_bytes=64)
-        ld = {}
+        w_code = once.tile([P, E], U32, align_bytes=64)
+        beta_rows = once.tile([P, E], BF16, align_bytes=64)
+        rows = {}
         for b in range(B):
-            for op in "kqx":
-                ld[op, b] = two.tile([P, 4, D], BF16, name=op + "_sb", align_bytes=64)
-            ld["v", b] = two.tile([P, 4, E], BF16, name="v_sb", align_bytes=64)
+            for name, width in (("k", D), ("q", D), ("x", D), ("v0", E)):
+                rows[name, b] = per_batch.tile([P, 4, width], BF16, name=name + "_rows", align_bytes=64)
 
-        def load(op, src, b, h):
-            order = "(t p) d -> p t d" if op in "qv" else "(p t) d -> p t d"
-            nc.sync.dma_start(
-                out=ld[op, b][:, 2 * h : 2 * h + 2, :], in_=src[b].rearrange(order, t=4)[:, 2 * h : 2 * h + 2, :]
-            )
+        def load(name, src, b, which):
+            view = src[b].rearrange("(p t) d -> p t d" if name in ("k", "x") else "(t p) d -> p t d", t=4)
+            nc.sync.dma_start(out=rows[name, b][:, which, :], in_=view[:, which, :])
 
-        nc.scalar.dma_start(out=rows[0:1, 0:S], in_=g.rearrange("(o s) -> o s", o=1))
-        nc.scalar.dma_start(out=rows[0:1, S : S + E], in_=beta.rearrange("(o s) -> o s", o=1))
-        for op, src in (("k", k), ("q", q), ("x", x)):
-            for h in (0, 1):
-                load(op, src, 0, h)
+        nc.scalar.dma_start(out=g_rows[0:1, :], in_=g.rearrange("(o s) -> o s", o=1))
+        first, second = slice(0, 2), slice(2, 4)
+        load("k", k, 0, slice(0, 1))
+        load("k", k, 0, slice(1, 2))
+        load("k", k, 0, second)
+        for name, src in (("q", q), ("x", x)):
+            load(name, src, 0, first)
+            load(name, src, 0, second)
         for Q in range(4):
             nc.sync.dma_start(
-                out=w_sc[32 * Q : 32 * Q + 4, :].bitcast(I32), in_=w_scales[0, 4 * Q : 4 * Q + 4, :].bitcast(I32)
+                out=w_scale[32 * Q : 32 * Q + 4, :].bitcast(I32), in_=w_scales[0, 4 * Q : 4 * Q + 4, :].bitcast(I32)
             )
-        nc.sync.dma_start(out=w_c[:].bitcast(I32), in_=w_words[0].rearrange("p n t -> p (n t)").bitcast(I32))
-        for op, src, b in (("k", k, 1), ("q", q, 1), ("v", v0, 0), ("x", x, 1), ("v", v0, 1)):
-            for h in (0, 1):
-                load(op, src, b, h)
+        nc.sync.dma_start(out=w_code[:].bitcast(I32), in_=w_words[0].rearrange("p n t -> p (n t)").bitcast(I32))
+        for name, src, b in (("k", k, 1), ("q", q, 1), ("x", x, 1), ("v0", v0, 0)):
+            load(name, src, b, first)
+            load(name, src, b, second)
+        nc.sync.dma_start(out=beta_rows[:], in_=beta.partition_broadcast(P))
+        load("v0", v0, 1, first)
+        load("v0", v0, 1, second)
 
-        pd = bank("pd")
-        for n in range(9):
-            nc.tensor.matmul(pd[:], lhsT=ones[:], rhs=zeros[:], start=True, stop=True)
-        for c in range(3):
-            pg = bank("pg")
-            nc.tensor.matmul(pg[:], lhsT=ones[:], rhs=rows[:, 512 * c : 512 * c + 512], start=True, stop=True)
-            if c == 0:
-                nc.scalar.activation(gb[:], pg[:], ACT.Copy, scale=float(S))
-            else:
-                nc.scalar.activation(bb[:, 512 * (c - 1) : 512 * c], pg[:], ACT.Copy, scale=1.0 / S)
-
-        codes = {}
+        quantised = {}
         for b in range(B):
-            for key, n in (("k", 512), ("q", 512), ("x", 512), ("a", 512), ("v", E)):
-                codes[key, b] = (
-                    two.tile([P, n], U32, name=key + "_c", align_bytes=64),
-                    two.tile([P, n], U8, name=key + "_s", align_bytes=64),
+            for name, columns in (
+                ("k", S),
+                ("q", S),
+                ("x", S),
+                ("a", S),
+                ("v", E),
+                ("y", 2 * S),
+            ):
+                quantised[name, b] = (
+                    per_batch.tile([P, columns], U32, name=name + "_code", align_bytes=64),
+                    per_batch.tile([P, columns], U8, name=name + "_scale", align_bytes=64),
                 )
-            codes["y", b] = (
-                two.tile([P, 2, 512], U32, name="y_c", align_bytes=64),
-                two.tile([P, 2, 512], U8, name="y_s", align_bytes=64),
-            )
-        st = {}
+        w = (w_code, w_scale)
+        made = {}
 
-        def copy(eng, out, in_):
-            if eng == "V":
+        def copy(engine, out, in_):
+            if engine == "V":
                 nc.vector.tensor_copy(out=out, in_=in_)
-            elif eng == "G":
-                nc.gpsimd.tensor_scalar(out, in_, 1.0, 1.0, op0=ALU.mult, op1=ALU.mult)
             else:
                 nc.scalar.copy(out=out, in_=in_)
 
-        def turn(words, name, eng, bufs):
-            pt = bank("p" + name)
-            ptv = pt[:].rearrange("p (a u r) -> p a u r", a=2, u=2)
-            for a in (0, 1):
+        def turn(engine, name, pairs, bufs=4):
+            turned = bank("turned")
+            blocks = turned[:].rearrange("p (m u r) -> p m u r", m=2, u=2)
+            for m in (0, 1):
                 for u in (0, 1):
-                    nc.tensor.transpose(ptv[:, a, u, :], words(a, u), ident[:])
-            gr = stage.tile([P, 256, 4], BF16, name=name, align_bytes=64, bufs=bufs)
-            o = gr[:].rearrange("p r t -> p (r t)").bitcast(F32).rearrange("p (a r u) -> p a r u", a=2, u=2)
-            copy(eng, o, ptv.rearrange("p a u r -> p a r u"))
-            return gr
+                    nc.tensor.transpose(blocks[:, m, u, :], pairs(m, u), identity[:])
+            slots = stream.tile([P, 256, 4], BF16, name=name, align_bytes=64, bufs=bufs)
+            copy(
+                engine,
+                slots[:].rearrange("p r s -> p (r s)").bitcast(F32).rearrange("p (m r u) -> p m r u", m=2, u=2),
+                blocks.rearrange("p m u r -> p m r u"),
+            )
+            return slots
 
-        def quant(dst, cs, src, pat):
+        def quantise(operand, columns, slots):
+            code, scale = operand
             nc.vector.quantize_mx(
-                out=dst[0][:, cs].bitcast(FP8X4), scales=dst[1][:, cs], in_=src[:].rearrange(pat)
+                out=code[:, columns].bitcast(FP8X4), scales=scale[:, columns], in_=slots[:].rearrange("p c s -> p (c s)")
             )
 
-        def mx(out, a, ac, b_, bc):
+        def multiply(out, left, left_columns, right, right_columns):
             nc.tensor.matmul_mx(
                 out=out,
-                lhsT=a[0][:, ac].bitcast(FP8X4),
-                lhsT_scale=a[1][:, ac],
-                rhs=b_[0][:, bc].bitcast(FP8X4),
-                rhs_scale=b_[1][:, bc],
+                lhsT=left[0][:, left_columns].bitcast(FP8X4),
+                lhsT_scale=left[1][:, left_columns],
+                rhs=right[0][:, right_columns].bitcast(FP8X4),
+                rhs_scale=right[1][:, right_columns],
                 start=True,
                 stop=True,
             )
 
-        def prep(op, b, h, eng):
-            src = ld[op, b]
-            st["g", op, b, h] = turn(lambda a, u: src[:, 2 * h + a, :].bitcast(F32)[:, u:256:2], "gr", eng, 6)
+        def part(width, n):
+            return slice(width * n, width * n + width)
 
-        def prepq(op, b, h):
-            quant(codes[op, b], slice(256 * h, 256 * h + 256), st["g", op, b, h], "p r t -> p (r t)")
+        def spread_g(engine):
+            gb = psum_g.tile([P, S], F32, name="gb")
+            nc.tensor.matmul(gb[:], lhsT=all_512[:], rhs=g_rows[:], start=True, stop=True)
+            made["gb"] = gb
 
-        def logits(b, T):
+        def turn_input(engine, name, b, h):
+            def pairs(m, u):
+                return rows[name, b][:, 2 * h + m, :].bitcast(F32)[:, u : D // 2 : 2]
+
+            made["turned", name, b, h] = turn(engine, "input_slots", pairs, bufs=6)
+
+        def quant_input(name, b, h):
+            quantise(quantised[name, b], part(256, h), made["turned", name, b, h])
+
+        def logits(engine, b, T):
             l = bank("l")
-            mx(l[:], codes["q", b], slice(128 * T, 128 * T + 128), codes["k", b], slice(0, 512))
-            m = stage.tile([P, 1], F32, name="m", bufs=8)
-            nc.vector.reduce_max(m[:], l[:], axis=AX.X)
-            nm = stage.tile([P, 1], F32, name="nm", bufs=8)
-            nc.scalar.activation(nm[:], m[:], ACT.Copy, scale=-SCALE)
-            st["l", b, T] = (l, nm)
+            multiply(l[:], quantised["q", b], part(P, T), quantised["k", b], part(S, 0))
+            top = stream.tile([P, 1], F32, name="top", bufs=ALL_TILES)
+            nc.vector.reduce_max(top[:], l[:], axis=AX.X)
+            shift = stream.tile([P, 1], F32, name="shift", bufs=ALL_TILES)
+            nc.scalar.activation(shift[:], top[:], ACT.Copy, scale=-(D**-0.5))
+            made["l", b, T] = (l, shift)
 
-        def expo(b, T):
-            l, nm = st["l", b, T]
-            e = stage.tile([P, 512], F32, name="e", align_bytes=64)
-            s = stage.tile([P, 1], F32, name="s", bufs=8)
-            nc.scalar.activation(e[:], l[:], ACT.Exp, bias=nm[:], scale=SCALE, accum_out=s[:])
-            st["e", b, T] = (e, s)
+        def exp(engine, b, T):
+            l, shift = made["l", b, T]
+            e = stream.tile([P, S], F32, name="e", align_bytes=64)
+            total = stream.tile([P, 1], F32, name="total", bufs=ALL_TILES)
+            nc.scalar.activation(e[:], l[:], ACT.Exp, bias=shift[:], scale=D**-0.5, accum_out=total[:])
+            made["e", b, T] = (e, total)
 
-        def norm(b, T, eng):
-            e, s = st["e", b, T]
-            r = stage.tile([P, 1], F32, name="r", bufs=8)
-            nc.vector.reciprocal(r[:], s[:])
-            w1 = stage.tile([P, 512], F32, name="w1", align_bytes=64)
-            if eng == "S":
-                nc.scalar.activation(w1[:], e[:], ACT.Identity, bias=minus[:], scale=r[:])
+        def norm(engine, b, T):
+            e, total = made["e", b, T]
+            r = stream.tile([P, 1], F32, name="r", bufs=ALL_TILES)
+            nc.vector.reciprocal(r[:], total[:])
+            centered = stream.tile([P, S], F32, name="centered", align_bytes=64)
+            if engine == "S":
+                nc.scalar.activation(centered[:], e[:], ACT.Identity, bias=minus[:], scale=r[:])
             else:
-                (nc.gpsimd if eng == "G" else nc.vector).tensor_scalar(
-                    w1[:], e[:], r[:], -1.0 / S, op0=ALU.mult, op1=ALU.add
-                )
-            st["w", b, T] = w1
+                nc.gpsimd.tensor_scalar(centered[:], e[:], r[:], -1.0 / S, op0=ALU.mult, op1=ALU.add)
+            made["centered", b, T] = centered
 
-        def shape(b, T, eng):
-            a = stage.tile([P, 512], BF16, name="a", align_bytes=64)
-            (nc.gpsimd if eng == "G" else nc.vector).tensor_tensor(
-                a[:].rearrange("i (u p e) -> i u p e", u=2, e=2),
-                st["w", b, T][:].rearrange("i (u e p) -> i u p e", u=2, e=2),
-                gb[:].rearrange("i (p u e) -> i u p e", u=2, e=2),
+        def shape(engine, b, T):
+            a = stream.tile([P, S], BF16, name="a", align_bytes=64)
+            nc.vector.tensor_tensor(
+                a[:].rearrange("i (u p z) -> i u p z", u=2, z=2),
+                made["centered", b, T][:].rearrange("i (u z p) -> i u p z", u=2, z=2),
+                made["gb"][:].rearrange("i (p u z) -> i u p z", u=2, z=2),
                 op=ALU.mult,
             )
-            st["a", b, T] = a
+            made["a", b, T] = a
 
-        def aturn(b, h, eng):
-            st["ga", b, h] = turn(
-                lambda a, u: st["a", b, 2 * h + a][:].bitcast(F32)[:, 128 * u : 128 * u + 128], "ga", eng, 4
-            )
+        def turn_a(engine, b, h):
+            def pairs(m, u):
+                return made["a", b, 2 * h + m][:].bitcast(F32)[:, part(P, u)]
 
-        def aquant(b, h):
-            quant(codes["a", b], slice(256 * h, 256 * h + 256), st["ga", b, h], "p r t -> p (r t)")
+            made["a_slots", b, h] = turn(engine, "a_slots", pairs)
 
-        def value(b, c, eng):
-            if ("gv", b, c // 4) not in st:
-                st["gv", b, c // 4] = stage.tile([P, 512, 4], BF16, name="gv", align_bytes=64)
-            gr = st["gv", b, c // 4]
-            pv = bank("pv")
-            pvv = pv[:].rearrange("p (t e) -> p t e", t=4)
+        def quant_a(engine, b, h):
+            quantise(quantised["a", b], part(256, h), made["a_slots", b, h])
+
+        def value(engine, b, c):
+            if c % 4 == 0:
+                made["v_slots", b, c // 4] = stream.tile([P, HALF, 4], BF16, name="v_slots", align_bytes=64)
+            v = bank("v")
             for t in range(4):
-                mx(pvv[:, t, :], codes["x", b], slice(128 * t, 128 * t + 128), (w_c, w_sc), slice(128 * c, 128 * c + 128))
-            copy(eng, gr[:, 128 * (c % 4) : 128 * (c % 4) + 128, :], pvv.rearrange("p t e -> p e t"))
+                multiply(v[:, part(P, t)], quantised["x", b], part(P, t), w, part(P, c))
+            copy(engine, made["v_slots", b, c // 4][:, part(P, c % 4), :], v[:].rearrange("p (t e) -> p e t", t=4))
 
-        def vquant(b, j):
-            quant(codes["v", b], slice(512 * j, 512 * j + 512), st["gv", b, j], "p e t -> p (e t)")
+        def quant_v(engine, b, h):
+            quantise(quantised["v", b], part(HALF, h), made["v_slots", b, h])
 
-        def attend(b, T, h):
-            po = bank("po")
-            mx(po[:], codes["a", b], slice(128 * T, 128 * T + 128), codes["v", b], slice(512 * h, 512 * h + 512))
-            t1 = stage.tile([P, 512], F32, name="t1", align_bytes=64, bufs=8)
-            nc.vector.tensor_tensor(t1[:], po[:], bb[:, 512 * h : 512 * h + 512], op=ALU.mult)
-            st["t1", b, T, h] = t1
-
-        def skip(b, T, h, eng):
-            R = stage.tile([P, 512], F32, name="R", align_bytes=64, bufs=8)
-            (nc.gpsimd if eng == "G" else nc.vector).tensor_tensor(
-                R[:], st["t1", b, T, h][:], ld["v", b][:, T, 512 * h : 512 * h + 512], op=ALU.add
+        def attend(engine, b, T, h):
+            o = bank("o")
+            multiply(o[:], quantised["a", b], part(P, T), quantised["v", b], part(HALF, h))
+            scaled = stream.tile([P, HALF], F32, name="scaled", align_bytes=64, bufs=HALF_TILES)
+            nc.vector.scalar_tensor_tensor(
+                scaled[:], o[:], 1.0 / S, beta_rows[:, part(HALF, h)], op0=ALU.mult, op1=ALU.mult
             )
-            st["R", b, T, h] = R
-            nc.sync.dma_start(out=out_0[b, 128 * T : 128 * T + 128, 512 * h : 512 * h + 512], in_=R[:])
+            made["scaled", b, T, h] = scaled
 
-        def cast(b, T, h, eng):
-            rb = stage.tile([P, 512], BF16, name="rb", align_bytes=64, bufs=8)
+        def skip(engine, b, T, h):
+            y = stream.tile([P, HALF], F32, name="y", align_bytes=64, bufs=HALF_TILES)
+            (nc.gpsimd if engine == "G" else nc.vector).tensor_tensor(
+                y[:], made["scaled", b, T, h][:], rows["v0", b][:, T, part(HALF, h)], op=ALU.add
+            )
+            made["y", b, T, h] = y
+            nc.sync.dma_start(out=out_0[b, part(P, T), part(HALF, h)], in_=y[:])
+
+        def round_y(engine, b, T, h):
+            rounded = stream.tile([P, HALF], BF16, name="rounded", align_bytes=64, bufs=HALF_TILES)
             copy(
-                eng,
-                rb[:].rearrange("i (u p e) -> i u p e", u=2, e=2),
-                st["R", b, T, h][:].rearrange("i (p u e) -> i u p e", u=2, e=2),
+                engine,
+                rounded[:].rearrange("i (u p z) -> i u p z", u=2, z=2),
+                made["y", b, T, h][:].rearrange("i (p u z) -> i u p z", u=2, z=2),
             )
-            st["rb", b, T, h] = rb
+            made["rounded", b, T, h] = rounded
 
-        def rturn(b, f, h, eng):
-            st["gy", b, f, h] = turn(
-                lambda a, u: st["rb", b, 2 * f + a, h][:].bitcast(F32)[:, 128 * u : 128 * u + 128], "gy", eng, 4
-            )
+        def turn_y(engine, b, f, h):
+            def pairs(m, u):
+                return made["rounded", b, 2 * f + m, h][:].bitcast(F32)[:, part(P, u)]
 
-        def yquant(b, f, h):
-            yc, ys = codes["y", b]
-            cs = slice(256 * f, 256 * f + 256)
-            nc.vector.quantize_mx(
-                out=yc[:, h, cs].bitcast(FP8X4), scales=ys[:, h, cs], in_=st["gy", b, f, h][:].rearrange("p r t -> p (r t)")
-            )
-            m0 = 512 * b + 256 * f
-            nc.sync.dma_start(
-                out=out_1[h, :, m0 : m0 + 256, :].rearrange("p m t -> p (m t)").bitcast(I32),
-                in_=yc[:, h, cs].bitcast(I32),
-            )
-            st["ny", b] = st.get(("ny", b), 0) + 1
-            if st["ny", b] == 4:
+            made["y_slots", b, f, h] = turn(engine, "y_slots", pairs)
+
+        def quant_y(engine, b, f, h):
+            code, scale = quantised["y", b]
+            quantise((code, scale), part(256, 2 * h + f), made["y_slots", b, f, h])
+            if b == B - 1 or f == 1:
+                start, count = (256 * f, 256) if b == B - 1 else (0, S)
+                nc.sync.dma_start(
+                    out=out_1[h, :, S * b + start : S * b + start + count, :].rearrange("p m t -> p (m t)").bitcast(I32),
+                    in_=code[:, S * h + start : S * h + start + count].bitcast(I32),
+                )
+            if f == 1 and h == 1:
                 for Q in range(4):
                     nc.sync.dma_start(
-                        out=out_2[:, 4 * Q : 4 * Q + 4, 512 * b : 512 * b + 512].rearrange("g q m -> q g m").bitcast(I32),
-                        in_=ys[32 * Q : 32 * Q + 4, :, :].bitcast(I32),
+                        out=out_2[:, 4 * Q : 4 * Q + 4, part(S, b)].rearrange("h q m -> q h m").bitcast(I32),
+                        in_=scale[32 * Q : 32 * Q + 4, :].rearrange("p (h m) -> p h m", h=2).bitcast(I32),
                     )
 
-        for f, b, i, j, eng in steps():
-            if f in ("pk", "pq", "px"):
-                prep(f[1], b, i, eng)
-            elif f in ("qk", "qq", "qx"):
-                prepq(f[1], b, i)
-            elif f == "l":
-                logits(b, i)
-            elif f == "x":
-                expo(b, i)
-            elif f == "n":
-                norm(b, i, eng)
-            elif f == "a":
-                shape(b, i, eng)
-            elif f == "at":
-                aturn(b, i, eng)
-            elif f == "aq":
-                aquant(b, i)
-            elif f == "vm":
-                value(b, i, eng)
-            elif f == "vq":
-                vquant(b, i)
-            elif f == "o":
-                attend(b, i, j)
-            elif f == "ad":
-                skip(b, i, j, eng)
-            elif f == "c":
-                cast(b, i, j, eng)
-            elif f == "rq":
-                yquant(b, i, j)
-            elif f == "rt":
-                rturn(b, i, j, eng)
+        steps = {
+            "spread_g": spread_g,
+            "logits": logits,
+            "exp": exp,
+            "norm": norm,
+            "shape": shape,
+            "turn_a": turn_a,
+            "quant_a": quant_a,
+            "value": value,
+            "quant_v": quant_v,
+            "attend": attend,
+            "skip": skip,
+            "round": round_y,
+            "turn_y": turn_y,
+            "quant_y": quant_y,
+        }
+        for name in ("k", "q", "x"):
+            steps["turn_" + name] = lambda engine, b, h, name=name: turn_input(engine, name, b, h)
+            steps["quant_" + name] = lambda engine, b, h, name=name: quant_input(name, b, h)
+        for entry in ORDER.replace("\n", " ").split(","):
+            fields = entry.split()
+            step = fields[0].split(":")
+            engine = step[1] if len(step) == 2 else ("V" if step[0] == "skip" else "S")
+            steps[step[0]](engine, *[int(n) for n in fields[1:]])

import math
from contextlib import ExitStack

import concourse.mybir as mybir
from concourse.masks import make_identity

F32 = mybir.dt.float32
BF16 = mybir.dt.bfloat16
U32 = mybir.dt.uint32
I32 = mybir.dt.int32
U8 = mybir.dt.uint8
FP8X4 = mybir.dt.float8_e4m3fn_x4
ALU = mybir.AluOpType
ACT = mybir.ActivationFunctionType
AX = mybir.AxisListType

B, S, D, E = 2, 512, 512, 1024
P = 128
HALF = 512
ALL_TILES = B * S // P
HALF_TILES = S // P * (E // HALF)
FLOPS = 2 * B * S * S * D + 2 * B * S * D * E + 2 * B * S * S * E

ORDER = """
    turn_k:V 0 0, turn_k:V 0 1, quant_k 0 0, turn_q 0 0, quant_k 0 1, quant_q 0 0, turn_q 0 1, turn_x 0 0,
    turn_x 0 1, quant_q 0 1, logits 0 0, exp 0 0, logits 0 1, logits 0 2, quant_x 0 0, norm:G 0 0, exp 0 1,
    exp 0 2, quant_x 0 1, turn_k:V 1 0, norm:G 0 1, turn_q 1 0, quant_k 1 0, spread_g, value 0 0, logits 0 3,
    value 0 1, norm:G 0 2, value 0 2, shape 0 0, shape 0 1, quant_q 1 0, turn_x:V 1 0, value 0 3, value:V 0 4,
    quant_x 1 0, turn_k 1 1, turn_q 1 1, quant_v 0 0, turn_x 1 1, quant_k 1 1, turn_a 0 0, exp 0 3,
    quant_q 1 1, value 0 5, value 0 6, value 0 7, shape 0 2, quant_x 1 1, quant_a 0 0, logits 1 0, norm:G 0 3,
    logits 1 1, attend 0 0 0, quant_v 0 1, value 1 0, exp 1 0, exp 1 1, value 1 1, shape 0 3, logits 1 2,
    value 1 2, skip:G 0 0 0, norm:G 1 0, exp 1 2, attend 0 0 1, norm 1 1, skip:G 0 0 1, logits 1 3,
    turn_a:V 0 1, attend 0 1 0, value 1 3, skip:G 0 1 0, quant_a 0 1, value 1 4, attend 0 1 1, exp 1 3,
    shape 1 0, value 1 5, shape 1 1, value 1 6, attend 0 2 0, attend 0 2 1, attend 0 3 0, turn_a 1 0,
    value 1 7, norm 1 2, norm 1 3, quant_v 1 0, quant_a 1 0, quant_v 1 1, shape 1 2, skip:G 0 1 1,
    skip:G 0 2 0, round 0 0 0, round 0 0 1, attend 1 0 0, round 0 1 0, skip:G 0 2 1, shape 1 3, attend 0 3 1,
    attend 1 0 1, skip:G 0 3 0, attend 1 1 0, round 0 1 1, skip:G 1 0 0, turn_a 1 1, quant_a 1 1, skip 1 0 1,
    skip:G 1 1 0, turn_y 0 0 0, attend 1 1 1, round 0 2 0, attend 1 2 0, attend 1 2 1, attend 1 3 0,
    round 1 0 0, round 0 2 1, round 1 0 1, attend 1 3 1, round 1 1 0, round 0 3 0, skip:G 0 3 1, skip 1 1 1,
    round 0 3 1, skip 1 2 0, turn_y 0 0 1, round 1 1 1, skip 1 2 1, turn_y 0 1 0, turn_y 0 1 1, quant_y 0 0 0,
    skip 1 3 0, quant_y 0 0 1, quant_y 0 1 0, quant_y 0 1 1, skip 1 3 1, round 1 2 0, round 1 2 1,
    round:V 1 3 0, round:V 1 3 1, turn_y 1 0 0, quant_y 1 0 0, turn_y 1 0 1, turn_y:V 1 1 0, turn_y 1 1 1,
    quant_y 1 0 1, quant_y 1 1 0, quant_y 1 1 1
"""


def tile_shapedcenteredattentionvalueskip_x2_kernel(
    tc, q, k, x, w_words, w_scales, g, beta, v0, out_0, out_1, out_2
):
    nc = tc.nc
    with ExitStack() as ctx:
        once = ctx.enter_context(tc.tile_pool(name="once", bufs=1))
        per_batch = ctx.enter_context(tc.tile_pool(name="per_batch", bufs=B))
        stream = ctx.enter_context(tc.tile_pool(name="stream", bufs=4))
        psum = ctx.enter_context(tc.psum_pool(name="psum", bufs=7))
        psum_g = ctx.enter_context(tc.psum_pool(name="psum_g", bufs=1))
        ctx.enter_context(tc.manual_schedule())

        def bank(name):
            return psum.tile([P, 512], F32, name=name, tag="bank")

        g_rows = once.tile([P, S], BF16, align_bytes=64)
        nc.vector.memset(g_rows[:], 0.0)
        w_scale = once.tile([P, E], U8, align_bytes=64)
        nc.vector.memset(w_scale[:].bitcast(I32), 0)
        one = once.tile([P, P], BF16, align_bytes=64)
        nc.vector.memset(one[:], 1.0)
        minus = once.tile([P, 1], F32)
        nc.vector.memset(minus[:], -1.0 / S)
        all_512 = once.tile([P, P], BF16, align_bytes=64)
        nc.scalar.activation(all_512[:], one[:], ACT.Exp, scale=math.log(S))
        identity = once.tile([P, P], F32, align_bytes=64)
        make_identity(nc, identity[:])

        w_code = once.tile([P, E], U32, align_bytes=64)
        beta_rows = once.tile([P, E], BF16, align_bytes=64)
        rows = {}
        for b in range(B):
            for name, width in (("k", D), ("q", D), ("x", D), ("v0", E)):
                rows[name, b] = per_batch.tile([P, 4, width], BF16, name=name + "_rows", align_bytes=64)

        def load(name, src, b, which):
            view = src[b].rearrange("(p t) d -> p t d" if name in ("k", "x") else "(t p) d -> p t d", t=4)
            nc.sync.dma_start(out=rows[name, b][:, which, :], in_=view[:, which, :])

        nc.scalar.dma_start(out=g_rows[0:1, :], in_=g.rearrange("(o s) -> o s", o=1))
        first, second = slice(0, 2), slice(2, 4)
        load("k", k, 0, slice(0, 1))
        load("k", k, 0, slice(1, 2))
        load("k", k, 0, second)
        for name, src in (("q", q), ("x", x)):
            load(name, src, 0, first)
            load(name, src, 0, second)
        for Q in range(4):
            nc.sync.dma_start(
                out=w_scale[32 * Q : 32 * Q + 4, :].bitcast(I32), in_=w_scales[0, 4 * Q : 4 * Q + 4, :].bitcast(I32)
            )
        nc.sync.dma_start(out=w_code[:].bitcast(I32), in_=w_words[0].rearrange("p n t -> p (n t)").bitcast(I32))
        for name, src, b in (("k", k, 1), ("q", q, 1), ("x", x, 1), ("v0", v0, 0)):
            load(name, src, b, first)
            load(name, src, b, second)
        nc.sync.dma_start(out=beta_rows[:], in_=beta.partition_broadcast(P))
        load("v0", v0, 1, first)
        load("v0", v0, 1, second)

        quantised = {}
        for b in range(B):
            for name, columns in (
                ("k", S),
                ("q", S),
                ("x", S),
                ("a", S),
                ("v", E),
                ("y", 2 * S),
            ):
                quantised[name, b] = (
                    per_batch.tile([P, columns], U32, name=name + "_code", align_bytes=64),
                    per_batch.tile([P, columns], U8, name=name + "_scale", align_bytes=64),
                )
        w = (w_code, w_scale)
        made = {}

        def copy(engine, out, in_):
            if engine == "V":
                nc.vector.tensor_copy(out=out, in_=in_)
            else:
                nc.scalar.copy(out=out, in_=in_)

        def turn(engine, name, pairs, bufs=4):
            turned = bank("turned")
            blocks = turned[:].rearrange("p (m u r) -> p m u r", m=2, u=2)
            for m in (0, 1):
                for u in (0, 1):
                    nc.tensor.transpose(blocks[:, m, u, :], pairs(m, u), identity[:])
            slots = stream.tile([P, 256, 4], BF16, name=name, align_bytes=64, bufs=bufs)
            copy(
                engine,
                slots[:].rearrange("p r s -> p (r s)").bitcast(F32).rearrange("p (m r u) -> p m r u", m=2, u=2),
                blocks.rearrange("p m u r -> p m r u"),
            )
            return slots

        def quantise(operand, columns, slots):
            code, scale = operand
            nc.vector.quantize_mx(
                out=code[:, columns].bitcast(FP8X4), scales=scale[:, columns], in_=slots[:].rearrange("p c s -> p (c s)")
            )

        def multiply(out, left, left_columns, right, right_columns):
            nc.tensor.matmul_mx(
                out=out,
                lhsT=left[0][:, left_columns].bitcast(FP8X4),
                lhsT_scale=left[1][:, left_columns],
                rhs=right[0][:, right_columns].bitcast(FP8X4),
                rhs_scale=right[1][:, right_columns],
                start=True,
                stop=True,
            )

        def part(width, n):
            return slice(width * n, width * n + width)

        def spread_g(engine):
            gb = psum_g.tile([P, S], F32, name="gb")
            nc.tensor.matmul(gb[:], lhsT=all_512[:], rhs=g_rows[:], start=True, stop=True)
            made["gb"] = gb

        def turn_input(engine, name, b, h):
            def pairs(m, u):
                return rows[name, b][:, 2 * h + m, :].bitcast(F32)[:, u : D // 2 : 2]

            made["turned", name, b, h] = turn(engine, "input_slots", pairs, bufs=6)

        def quant_input(name, b, h):
            quantise(quantised[name, b], part(256, h), made["turned", name, b, h])

        def logits(engine, b, T):
            l = bank("l")
            multiply(l[:], quantised["q", b], part(P, T), quantised["k", b], part(S, 0))
            top = stream.tile([P, 1], F32, name="top", bufs=ALL_TILES)
            nc.vector.reduce_max(top[:], l[:], axis=AX.X)
            shift = stream.tile([P, 1], F32, name="shift", bufs=ALL_TILES)
            nc.scalar.activation(shift[:], top[:], ACT.Copy, scale=-(D**-0.5))
            made["l", b, T] = (l, shift)

        def exp(engine, b, T):
            l, shift = made["l", b, T]
            e = stream.tile([P, S], F32, name="e", align_bytes=64)
            total = stream.tile([P, 1], F32, name="total", bufs=ALL_TILES)
            nc.scalar.activation(e[:], l[:], ACT.Exp, bias=shift[:], scale=D**-0.5, accum_out=total[:])
            made["e", b, T] = (e, total)

        def norm(engine, b, T):
            e, total = made["e", b, T]
            r = stream.tile([P, 1], F32, name="r", bufs=ALL_TILES)
            nc.vector.reciprocal(r[:], total[:])
            centered = stream.tile([P, S], F32, name="centered", align_bytes=64)
            if engine == "S":
                nc.scalar.activation(centered[:], e[:], ACT.Identity, bias=minus[:], scale=r[:])
            else:
                nc.gpsimd.tensor_scalar(centered[:], e[:], r[:], -1.0 / S, op0=ALU.mult, op1=ALU.add)
            made["centered", b, T] = centered

        def shape(engine, b, T):
            a = stream.tile([P, S], BF16, name="a", align_bytes=64)
            nc.vector.tensor_tensor(
                a[:].rearrange("i (u p z) -> i u p z", u=2, z=2),
                made["centered", b, T][:].rearrange("i (u z p) -> i u p z", u=2, z=2),
                made["gb"][:].rearrange("i (p u z) -> i u p z", u=2, z=2),
                op=ALU.mult,
            )
            made["a", b, T] = a

        def turn_a(engine, b, h):
            def pairs(m, u):
                return made["a", b, 2 * h + m][:].bitcast(F32)[:, part(P, u)]

            made["a_slots", b, h] = turn(engine, "a_slots", pairs)

        def quant_a(engine, b, h):
            quantise(quantised["a", b], part(256, h), made["a_slots", b, h])

        def value(engine, b, c):
            if c % 4 == 0:
                made["v_slots", b, c // 4] = stream.tile([P, HALF, 4], BF16, name="v_slots", align_bytes=64)
            v = bank("v")
            for t in range(4):
                multiply(v[:, part(P, t)], quantised["x", b], part(P, t), w, part(P, c))
            copy(engine, made["v_slots", b, c // 4][:, part(P, c % 4), :], v[:].rearrange("p (t e) -> p e t", t=4))

        def quant_v(engine, b, h):
            quantise(quantised["v", b], part(HALF, h), made["v_slots", b, h])

        def attend(engine, b, T, h):
            o = bank("o")
            multiply(o[:], quantised["a", b], part(P, T), quantised["v", b], part(HALF, h))
            scaled = stream.tile([P, HALF], F32, name="scaled", align_bytes=64, bufs=HALF_TILES)
            nc.vector.scalar_tensor_tensor(
                scaled[:], o[:], 1.0 / S, beta_rows[:, part(HALF, h)], op0=ALU.mult, op1=ALU.mult
            )
            made["scaled", b, T, h] = scaled

        def skip(engine, b, T, h):
            y = stream.tile([P, HALF], F32, name="y", align_bytes=64, bufs=HALF_TILES)
            (nc.gpsimd if engine == "G" else nc.vector).tensor_tensor(
                y[:], made["scaled", b, T, h][:], rows["v0", b][:, T, part(HALF, h)], op=ALU.add
            )
            made["y", b, T, h] = y
            nc.sync.dma_start(out=out_0[b, part(P, T), part(HALF, h)], in_=y[:])

        def round_y(engine, b, T, h):
            rounded = stream.tile([P, HALF], BF16, name="rounded", align_bytes=64, bufs=HALF_TILES)
            copy(
                engine,
                rounded[:].rearrange("i (u p z) -> i u p z", u=2, z=2),
                made["y", b, T, h][:].rearrange("i (p u z) -> i u p z", u=2, z=2),
            )
            made["rounded", b, T, h] = rounded

        def turn_y(engine, b, f, h):
            def pairs(m, u):
                return made["rounded", b, 2 * f + m, h][:].bitcast(F32)[:, part(P, u)]

            made["y_slots", b, f, h] = turn(engine, "y_slots", pairs)

        def quant_y(engine, b, f, h):
            code, scale = quantised["y", b]
            quantise((code, scale), part(256, 2 * h + f), made["y_slots", b, f, h])
            if b == B - 1 or f == 1:
                start, count = (256 * f, 256) if b == B - 1 else (0, S)
                nc.sync.dma_start(
                    out=out_1[h, :, S * b + start : S * b + start + count, :].rearrange("p m t -> p (m t)").bitcast(I32),
                    in_=code[:, S * h + start : S * h + start + count].bitcast(I32),
                )
            if f == 1 and h == 1:
                for Q in range(4):
                    nc.sync.dma_start(
                        out=out_2[:, 4 * Q : 4 * Q + 4, part(S, b)].rearrange("h q m -> q h m").bitcast(I32),
                        in_=scale[32 * Q : 32 * Q + 4, :].rearrange("p (h m) -> p h m", h=2).bitcast(I32),
                    )

        steps = {
            "spread_g": spread_g,
            "logits": logits,
            "exp": exp,
            "norm": norm,
            "shape": shape,
            "turn_a": turn_a,
            "quant_a": quant_a,
            "value": value,
            "quant_v": quant_v,
            "attend": attend,
            "skip": skip,
            "round": round_y,
            "turn_y": turn_y,
            "quant_y": quant_y,
        }
        for name in ("k", "q", "x"):
            steps["turn_" + name] = lambda engine, b, h, name=name: turn_input(engine, name, b, h)
            steps["quant_" + name] = lambda engine, b, h, name=name: quant_input(name, b, h)
        for entry in ORDER.replace("\n", " ").split(","):
            fields = entry.split()
            step = fields[0].split(":")
            engine = step[1] if len(step) == 2 else ("V" if step[0] == "skip" else "S")
            steps[step[0]](engine, *[int(n) for n in fields[1:]])
